import numpy as np
import ml_dtypes


def mxq(x, axis, fmt="e4m3"):
    dtype, down = {"e4m3": (ml_dtypes.float8_e4m3fn, 7), "e5m2": (ml_dtypes.float8_e5m2, 14)}[fmt]
    v = np.moveaxis(np.asarray(x, np.float32).astype(ml_dtypes.bfloat16).astype(np.float64), axis, -1)
    blocks = v.reshape(v.shape[:-1] + (-1, 32))
    amax = np.abs(blocks).max(-1, keepdims=True)
    byte = np.maximum(np.where(amax > 0, np.frexp(amax)[1] - 1 + 127, 0) - down, 1)
    scale = np.exp2(byte - 127.0)
    codes = (blocks / scale).astype(np.float32).astype(dtype).astype(np.float64)
    return np.moveaxis((codes * scale).reshape(v.shape), -1, axis)


WIDE = False


def mx_kscale(k):
    if not WIDE:
        return np.ones(k)
    levels = np.array([10, -10, 5, -5, 0])
    if k % 512:
        return np.exp2(np.random.permutation(np.resize(levels, k // 32))).repeat(32)
    a = np.empty((k // 512, 16))
    for p in range(k // 512):
        a[p, :8] = np.random.permutation(np.resize(levels, 8))
        for g in range(8):
            far = levels[np.abs(levels - a[p, g]) >= 10]
            a[p, g + 8] = far[np.random.randint(len(far))]
    return np.exp2(a.ravel()).repeat(32)


BF16 = ml_dtypes.bfloat16


def bf(x):
    return np.asarray(x, np.float32).astype(BF16)


def f64(x):
    return np.asarray(x).astype(np.float64)


E2M1 = np.array([0.0, 0.5, 1.0, 1.5, 2.0, 3.0, 4.0, 6.0, -0.0, -0.5, -1.0, -1.5, -2.0, -3.0, -4.0, -6.0])


def pack_weight(w, fmt):
    k, n = w.shape
    w = f64(bf(w)).reshape(k // 32, 32, n)
    amax = np.abs(w).max(1)
    if fmt == "e4m3":
        byte = np.frexp(amax)[1] - 1 + 127 - 7
    else:
        mant, ex = np.frexp(amax / 6.0)
        byte = np.where(mant > 0.5, ex, ex - 1) + 127
    byte = np.clip(np.where(amax > 0, byte, 1), 1, 254)
    scaled = (w * np.exp2(127.0 - byte)[:, None, :]).reshape(k, n).astype(np.float32)
    by_word = np.ascontiguousarray(scaled.reshape(k // 512, 128, 4, n).transpose(0, 1, 3, 2))
    if fmt == "e4m3":
        words = by_word.astype(ml_dtypes.float8_e4m3fn).view(np.uint8)
    else:
        c = by_word.astype(ml_dtypes.float4_e2m1fn).view(np.uint8) & 0xF
        words = c[..., 0::2] | (c[..., 1::2] << 4)
    return np.ascontiguousarray(words), np.ascontiguousarray(byte.astype(np.uint8).reshape(k // 512, 16, n))


def unpack_weight(words, scales, fmt):
    g, p, n, _ = words.shape
    if fmt == "e4m3":
        vals = np.ascontiguousarray(words).view(ml_dtypes.float8_e4m3fn).astype(np.float64)
    else:
        nib = np.empty((g, p, n, 4), np.uint8)
        nib[..., 0::2] = words & 0xF
        nib[..., 1::2] = words >> 4
        vals = E2M1[nib]
    vals = vals * np.repeat(np.exp2(scales.astype(np.float64) - 127.0), 8, axis=1)[..., None]
    return vals.transpose(0, 1, 3, 2).reshape(g * 512, n)
def pack4(w):
    words, scales = pack_weight(w, "e2m1")
    return words.reshape(words.shape[0], 128, -1), scales


def unpack4(words, scales):
    return unpack_weight(words.reshape(words.shape[0], 128, -1, 2), scales, "e2m1")


M, D, V, R = 1024, 1024, 2048, 512


def draw0():
    s, t, r = mx_kscale(D), mx_kscale(V), mx_kscale(M)
    base = np.random.standard_normal((D, V))
    u_words, u_scales = pack4(base.T / np.sqrt(V) / t[:, None])
    return {"hid": bf(np.random.standard_normal((M, D)) * s),
            "w": bf(base / np.sqrt(D) / s[:, None]),
            "teach": bf(0.7 * np.random.standard_normal((M, V))),
            "centre": bf(0.3 * np.random.standard_normal(M)),
            "probs": bf(np.exp(0.5 * np.random.standard_normal((M, V))) * t * r[:, None]),
            "u_words": u_words, "u_scales": u_scales,
            "act": bf(np.random.standard_normal((M, R)) / np.sqrt(M) / r[:, None])}


def core(hid, w, teach, centre, probs, u_words, u_scales, act):
    z = mxq(f64(hid), 1, "e4m3") @ mxq(f64(w), 0, "e4m3")
    e = f64(probs) * (z - f64(teach) - f64(centre)[:, None])
    dhid = mxq(e, 1, "e4m3") @ unpack4(u_words, u_scales)
    dup = mxq(f64(act), 0, "e4m3").T @ mxq(e, 0, "e4m3")
    return dhid, dup


def e4m3fn_bytes(y):
    return np.clip(np.asarray(y, np.float64), -448.0, 448.0).astype(np.float32).astype(ml_dtypes.float8_e4m3fn).view(np.uint8)


def e4m3fn_values(b):
    return np.asarray(b, np.uint8).view(ml_dtypes.float8_e4m3fn).astype(np.float64)


def setup_inputs():
    d = draw0()
    x0 = np.asarray(d['w']).astype(np.float64)
    s = (np.max(np.abs(x0), axis=(1,), keepdims=True) / 448.0).astype(np.float32)
    out = {}
    for k, v in d.items():
        if k == 'w':
            out['w_bytes'] = e4m3fn_bytes(x0 / s.astype(np.float64))
            out['w_scale'] = s
        else:
            out[k] = v
    return out


def reference(hid, w_bytes, w_scale, teach, centre, probs, u_words, u_scales, act):
    return core(hid, e4m3fn_values(w_bytes) * w_scale.astype(np.float64), teach, centre, probs, u_words, u_scales, act)

@@ -1,0 +1,507 @@
+from contextlib import ExitStack
+
+import concourse.mybir as mybir
+from concourse.masks import make_identity
+
+F32 = mybir.dt.float32
+BF16 = mybir.dt.bfloat16
+U32 = mybir.dt.uint32
+I32 = mybir.dt.int32
+U8 = mybir.dt.uint8
+FP8 = mybir.dt.float8_e4m3fn
+FP8X4 = mybir.dt.float8_e4m3fn_x4
+FP4X4 = mybir.dt.float4_e2m1fn_x4
+ALU = mybir.AluOpType
+ACT = mybir.ActivationFunctionType
+
+M, D, V, R = 1024, 1024, 2048, 512
+P = 128
+C = 512
+FLOPS = 2 * M * D * V * 2 + 2 * M * R * V
+STEPS = 16
+Z_BANKS = 3
+TOK_ON_VECTOR = 256
+ON_GPSIMD = 128
+RUN = 8
+
+
+def tile_reverse_kl_backward_s8_kernel(
+    tc, hid, w_bytes, w_scale, teach, centre, probs, u_words, u_scales, act, out_0, out_1
+):
+    nc = tc.nc
+    with ExitStack() as ctx:
+        keep = ctx.enter_context(tc.tile_pool(name="keep", bufs=1))
+        work = ctx.enter_context(tc.tile_pool(name="work", bufs=2))
+        psum = ctx.enter_context(tc.psum_pool(name="psum", bufs=1))
+        ctx.enter_context(tc.manual_schedule())
+
+        wsc = keep.tile([P, 8], F32, name="wsc")
+        cen = keep.tile([P, 8], BF16, name="cen")
+        cen32 = keep.tile([P, 8], F32, name="cen32")
+        ident = keep.tile([P, P], F32, name="ident")
+        u_codes = keep.tile([P, 4, 2 * D], U8, name="u_codes", align_bytes=64)
+        u_sc = keep.tile([P, 4, D], U8, name="u_sc", align_bytes=64)
+
+        def mx_tiles(pool, name, width, bufs):
+            codes = pool.tile([P, width], U32, name=name + "_codes", align_bytes=64, bufs=bufs)
+            scales = pool.tile([P, width], U8, name=name + "_scales", align_bytes=64, bufs=bufs)
+            return codes, scales
+
+        def quantise(mx, src, a, b):
+            nc.vector.quantize_mx(out=mx[0][:, a:b].bitcast(FP8X4), scales=mx[1][:, a:b], in_=src[:, 4 * a : 4 * b])
+
+        def bank(name):
+            return psum.tile([P, C], F32, name=name)
+
+        nc.scalar.dma_start(
+            out=wsc[:].rearrange("p (g t) -> p g t", t=4), in_=w_scale.rearrange("(g p t) o -> p g (t o)", p=P, t=4)
+        )
+        nc.scalar.dma_start(out=cen[:].rearrange("p (g t) -> p g t", t=4), in_=centre.rearrange("(g p t) -> p g t", p=P, t=4))
+        nc.scalar.activation(out=cen32[:], in_=cen[:], func=ACT.Copy)
+        make_identity(nc, ident[:])
+        nc.gpsimd.memset(u_sc[:].rearrange("p g n -> p (g n)").bitcast(I32), 0)
+
+        w_view = w_bytes.rearrange("(g p t) v -> g p t v", p=P, t=4)
+        w_raw = {}
+
+        def load_w(kg, c, n):
+            wb = keep.tile([P, 4, n * C], U8, name="w_bytes_%d_%d" % (kg, c))
+            nc.sync.dma_start(out=wb[:], in_=w_view[kg][:, :, c * C : (c + n) * C])
+            for i in range(n):
+                w_raw[kg, c + i] = wb[:, :, i * C : (i + 1) * C]
+
+        def slots(src, j):
+            g, h = divmod(j, 2)
+            return src[g * C : (g + 1) * C, :].rearrange("(p t) x -> p t x", t=4)[:, 2 * h : 2 * h + 2, :]
+
+        hid_rows = {}
+
+        def load_hid(j):
+            hid_rows[j] = work.tile([P, 2 * D], BF16, name="rows", bufs=4)
+            nc.sync.dma_start(out=hid_rows[j][:].rearrange("p (t d) -> p t d", t=2), in_=slots(hid, j))
+
+        act_rows = {}
+
+        def load_act(g):
+            act_rows[g] = work.tile([P, 4 * R], BF16, name="rows", bufs=4)
+            nc.sync.dma_start(out=act_rows[g][:], in_=act[g * C : (g + 1) * C, :].rearrange("(p t) r -> p (t r)", t=4))
+
+        te = {(g, c): keep.tile([P, 4 * C], BF16, name="te_%d_%d" % (g, c)) for g in range(2) for c in range(4)}
+        pr = {(g, c): keep.tile([P, 4 * C], BF16, name="pr_%d_%d" % (g, c)) for g in range(2) for c in range(4)}
+
+        def load_tp(s):
+            j, c = divmod(s, 4)
+            g, h = divmod(j, 2)
+            for dst, src in ((te, teach), (pr, probs)):
+                nc.sync.dma_start(
+                    out=dst[g, c][:, 2 * h * C : (2 * h + 2) * C].rearrange("p (t v) -> p t v", t=2),
+                    in_=slots(src, j)[:, :, c * C : (c + 1) * C],
+                )
+
+        load_w(0, 0, 1)
+        load_w(1, 0, 1)
+        load_hid(0)
+        load_w(0, 1, 1)
+        load_w(1, 1, 1)
+        load_tp(0)
+        load_hid(1)
+        load_w(0, 2, 2)
+        load_w(1, 2, 2)
+        load_hid(3)
+        load_tp(1)
+        load_hid(2)
+        for q in range(4):
+            nc.sync.dma_start(
+                out=u_sc[32 * q : 32 * q + 4, :, :].bitcast(I32),
+                in_=u_scales[:, 4 * q : 4 * q + 4, :].rearrange("g q n -> q g n").bitcast(I32),
+            )
+        nc.sync.dma_start(out=u_codes[:], in_=u_words.rearrange("g p b -> p g b"))
+        load_tp(2)
+        load_tp(3)
+        load_act(0)
+        load_tp(4)
+        load_act(1)
+        for s in range(5, STEPS):
+            load_tp(s)
+
+        wide = {}
+
+        def widen(kg, c, engines):
+            if (kg, c) not in wide:
+                wide[kg, c] = work.tile([P, 4, C], BF16, name="wide", bufs=4)
+            for t in range(4):
+                if engines[t] == "-":
+                    continue
+                src = w_raw[kg, c][:, t, :].bitcast(FP8)
+                sc = wsc[:, 4 * kg + t : 4 * kg + t + 1]
+                if engines[t] == "S":
+                    nc.scalar.activation(out=wide[kg, c][:, t, :], in_=src, func=ACT.Copy, scale=sc)
+                else:
+                    nc.vector.tensor_scalar(out=wide[kg, c][:, t, :], in0=src, scalar1=sc, scalar2=None, op0=ALU.mult)
+
+        def interleave(dst, src, engine, a, b):
+            o = dst[:, 4 * a : 4 * b].rearrange("p (c i t) -> p c t i", i=RUN, t=4)
+            s = src[:, :, a:b].rearrange("p t (c i) -> p c t i", i=RUN)
+            if engine == "V":
+                nc.vector.tensor_copy(out=o, in_=s)
+            elif engine == "S":
+                nc.scalar.copy(out=o, in_=s)
+            else:
+                nc.gpsimd.tensor_scalar(
+                    out=dst[:, 4 * a : 4 * b].rearrange("p (c t) -> p c t", t=4),
+                    in0=src[:, :, a:b].rearrange("p t c -> p c t"),
+                    scalar1=1.0,
+                    scalar2=0.0,
+                    op0=ALU.mult,
+                    op1=ALU.add,
+                )
+
+        woven = {}
+
+        def weave(key, src, engine, a=0, b=C):
+            if key not in woven:
+                woven[key] = work.tile([P, 4 * C], BF16, name="woven", align_bytes=64, bufs=5)
+            interleave(woven[key], src, engine, a, b)
+
+        w_mx = {(kg, c): mx_tiles(keep, "w_%d_%d" % (kg, c), C, 1) for kg in range(2) for c in range(4)}
+        hid_mx = {j: mx_tiles(keep, "hid_%d" % j, C, 1) for j in range(4)}
+        act_mx = {g: mx_tiles(keep, "act_%d" % g, R, 1) for g in range(2)}
+
+        def w_weave(kg, c, engine="V", a=0, b=C):
+            weave(("w", kg, c), wide[kg, c][:], engine, a, b)
+
+        def w_quant(kg, c):
+            quantise(w_mx[kg, c], woven["w", kg, c], 0, C)
+
+        def turn(b, words):
+            for i, w in enumerate(words):
+                nc.tensor.transpose(b[:, i * P : (i + 1) * P], w, ident[:])
+
+        def unturn(dst, b):
+            nc.scalar.copy(
+                out=dst.bitcast(F32).rearrange("q (t p u) -> q t p u", t=2, u=2),
+                in_=b[:].rearrange("q (t u p) -> q t p u", t=2, u=2),
+            )
+
+        hid_t = {}
+
+        turned = {}
+
+        def hid_turn(j, kg, name):
+            words = hid_rows[j][:].bitcast(F32)
+            turned["hid", j, kg] = b = bank(name)
+            turn(b, [words[:, t * C + kg * 2 * P + u : t * C + (kg + 1) * 2 * P : 2] for t in range(2) for u in range(2)])
+
+        def hid_unturn(j, kg):
+            if kg == 0:
+                hid_t[j] = work.tile([P, 4 * C], BF16, name="hid_t", align_bytes=64, bufs=2)
+            unturn(hid_t[j][:, kg * 2 * C : (kg + 1) * 2 * C], turned["hid", j, kg])
+
+        def hid_quant(j):
+            quantise(hid_mx[j], hid_t[j], 0, C)
+
+        def where(n):
+            s, i = divmod(n, 2)
+            j, c = divmod(s, 4)
+            return j, i, j // 2, 2 * (j % 2) + i, c
+
+        zb = {}
+
+        def z_bank(n):
+            return "z%d" % (n % Z_BANKS if n >= 6 else n % 2)
+
+        def z_mm(n):
+            j, i, g, t, c = where(n)
+            zb[n] = bank(z_bank(n))
+            for kg in range(2):
+                cols = slice((2 * kg + i) * P, (2 * kg + i + 1) * P)
+                nc.tensor.matmul_mx(
+                    out=zb[n][:],
+                    lhsT=hid_mx[j][0][:, cols].bitcast(FP8X4),
+                    lhsT_scale=hid_mx[j][1][:, cols],
+                    rhs=w_mx[kg, c][0][:].bitcast(FP8X4),
+                    rhs_scale=w_mx[kg, c][1][:],
+                    start=kg == 0,
+                    stop=kg == 1,
+                )
+
+        diff = {}
+
+        def subtract(n):
+            j, i, g, t, c = where(n)
+            if i == 0:
+                diff[n // 2] = work.tile([P, 2 * C], F32, name="diff", bufs=2)
+            nc.vector.scalar_tensor_tensor(
+                out=diff[n // 2][:, i * C : (i + 1) * C],
+                in0=zb[n][:],
+                scalar=cen32[:, 4 * g + t : 4 * g + t + 1],
+                in1=te[g, c][:, t * C : (t + 1) * C],
+                op0=ALU.subtract,
+                op1=ALU.subtract,
+            )
+
+        def multiply(s, a=0, b=2):
+            j, i, g, t, c = where(2 * s)
+            cols = slice(t * C, (t + 2) * C)
+            nc.vector.tensor_tensor(
+                out=te[g, c][:, cols].rearrange("p (t u x) -> p u t x", u=2, t=2)[:, a:b],
+                in0=diff[s][:].rearrange("p (x u e) -> p u x e", u=2, e=2)[:, a:b],
+                in1=pr[g, c][:, cols].rearrange("p (x u e) -> p u x e", u=2, e=2)[:, a:b],
+                op=ALU.mult,
+            )
+
+        e_t = {}
+        voc_mx = {}
+
+        def e_turn(s):
+            j, i, g, t, c = where(2 * s)
+            words = te[g, c][:].bitcast(F32)
+            turned["e", s] = b = bank("t0")
+            turn(b, [words[:, (2 * t + x) * P : (2 * t + x + 1) * P] for x in range(4)])
+
+        def e_unturn(s):
+            e_t[s] = work.tile([P, 2 * C], BF16, name="e_t", align_bytes=64, bufs=3)
+            unturn(e_t[s][:], turned["e", s])
+
+        def voc_quant(s):
+            voc_mx[s] = mx_tiles(work, "voc", 2 * P, 6)
+            quantise(voc_mx[s], e_t[s], 0, 2 * P)
+
+        def dhid_pass(b, s, i, nh):
+            c = s % 4
+            nc.tensor.matmul_mx(
+                out=b[:],
+                lhsT=voc_mx[s][0][:, i * P : (i + 1) * P].bitcast(FP8X4),
+                lhsT_scale=voc_mx[s][1][:, i * P : (i + 1) * P],
+                rhs=u_codes[:, c, nh * 2 * C : (nh + 1) * 2 * C].bitcast(FP4X4),
+                rhs_scale=u_sc[:, c, nh * C : (nh + 1) * C],
+                start=c == 0,
+                stop=c == 3,
+            )
+
+        def copy_out(engine, src, dst, shape):
+            r = work.tile([P, C], F32, name="res", bufs=6)
+            if engine == "S":
+                nc.scalar.copy(out=shape(r[:]), in_=src)
+            else:
+                nc.vector.tensor_copy(out=shape(r[:]), in_=src)
+            nc.sync.dma_start(out=dst, in_=r[:])
+
+        def dhid_out(engine, b, j, i, nh):
+            copy_out(engine, b[:], slots(out_0, j)[:, i, nh * C : (nh + 1) * C], lambda r: r)
+
+        groups = [(i, nh) for i in range(2) for nh in range(2)]
+        held = {}
+
+        def dhid_step(s, a=0, b=4):
+            for x in range(a, b):
+                i, nh = groups[x]
+                if s % 4 == 0:
+                    held[x] = bank("d%d" % x)
+                dhid_pass(held[x], s, i, nh)
+
+        def dhid_outs(j, engines):
+            for x, (i, nh) in enumerate(groups):
+                dhid_out(engines[x], held[x], j, i, nh)
+
+        tok_mx = {}
+
+        def tok_weave(g, c, engine, a=0, b=C):
+            weave(("tok", g, c), te[g, c][:].rearrange("p (t v) -> p t v", t=4), engine, a, b)
+
+        def tok_quant(g, c):
+            tok_mx[g, c] = mx_tiles(work, "tok", C, 6)
+            quantise(tok_mx[g, c], woven["tok", g, c], 0, C)
+
+        def act_weave(g, engine, a=0, b=R):
+            weave(("act", g), act_rows[g][:].rearrange("p (t r) -> p t r", t=4), engine, a, b)
+
+        def act_quant(g):
+            quantise(act_mx[g], woven["act", g], 0, R)
+
+        dup_b = {}
+
+        def dup(name, r, c):
+            dup_b[r, c] = b = bank(name)
+            for g in range(2):
+                nc.tensor.matmul_mx(
+                    out=b[:],
+                    lhsT=act_mx[g][0][:, r * P : (r + 1) * P].bitcast(FP8X4),
+                    lhsT_scale=act_mx[g][1][:, r * P : (r + 1) * P],
+                    rhs=tok_mx[g, c][0][:].bitcast(FP8X4),
+                    rhs_scale=tok_mx[g, c][1][:],
+                    start=g == 0,
+                    stop=g == 1,
+                )
+
+        def dup_out(engine, r, c):
+            copy_out(
+                engine,
+                dup_b[r, c][:].rearrange("p (u q e) -> p q u e", u=2, e=2),
+                out_1[r * P : (r + 1) * P, c * C : (c + 1) * C],
+                lambda x: x.rearrange("p (q u e) -> p q u e", u=2, e=2),
+            )
+
+        hid_turn(0, 0, "d0")
+        hid_turn(0, 1, "d1")
+        widen(0, 0, "VVVV")
+        widen(1, 0, "VVSS")
+        w_weave(0, 0)
+        w_weave(1, 0)
+        widen(0, 1, "S---")
+        hid_unturn(0, 0)
+        hid_unturn(0, 1)
+        w_quant(0, 0)
+        w_quant(1, 0)
+        widen(0, 1, "-SSS")
+        hid_quant(0)
+        z_mm(0)
+        z_mm(1)
+        hid_turn(1, 0, "d2")
+        hid_turn(1, 1, "d3")
+        widen(1, 1, "VVSS")
+        w_weave(0, 1)
+        w_weave(1, 1, "G", 0, ON_GPSIMD)
+
+        widen(0, 2, "SSSS")
+        hid_unturn(1, 0)
+        hid_unturn(1, 1)
+        widen(1, 2, "SSS-")
+        for s in range(3):
+            c = s + 1
+            subtract(2 * s)
+            subtract(2 * s + 1)
+            if c < 3:
+                w_weave(1, c, "V", ON_GPSIMD, C)
+            w_quant(0, c)
+            w_quant(1, c)
+            multiply(s)
+            z_mm(2 * c)
+            z_mm(2 * c + 1)
+            if s == 2:
+                hid_turn(2, 1, "t0")
+                hid_unturn(2, 1)
+                voc_quant(1)
+                dhid_step(0, 2, 4)
+                dhid_step(1)
+            e_turn(s)
+            if s == 0:
+                widen(0, 3, "SSSS")
+                e_unturn(0)
+                for kg in range(2):
+                    hid_turn(3, kg, "d%d" % (2 + kg))
+                widen(1, 3, "SSS-")
+                w_weave(0, 3, "S")
+                hid_quant(1)
+                widen(1, 2, "---V")
+                w_weave(0, 2)
+                w_weave(1, 2, "G", 0, ON_GPSIMD)
+            if s == 1:
+                widen(1, 3, "---V")
+                voc_quant(0)
+                hid_turn(2, 0, "z2")
+                dhid_step(0, 0, 2)
+                w_weave(1, 3, "G", 0, ON_GPSIMD)
+                w_weave(1, 3, "S", ON_GPSIMD, C)
+                e_unturn(1)
+                for kg in range(2):
+                    hid_unturn(3, kg)
+                hid_unturn(2, 0)
+            if s == 2:
+                act_weave(0, "S")
+                e_unturn(2)
+        z_mm(8)
+
+        for s in range(3, 12):
+            j, c = divmod(s, 4)
+            for n in (2 * s, 2 * s + 1):
+                subtract(n)
+                z_mm(n + Z_BANKS)
+            if s > 3:
+                e_turn(s - 1)
+                e_unturn(s - 1)
+            if s > 3:
+                voc_quant(s - 2)
+            else:
+                hid_quant(3)
+            multiply(s)
+            if s == 3:
+                hid_quant(2)
+            if s > 3:
+                dhid_step(s - 2)
+                if s % 4 == 1:
+                    dhid_outs(s // 4 - 1, "SSSS")
+            if s == 3:
+                act_weave(1, "S")
+            if s in (6, 7, 8):
+                tok_weave(0, s - 6, "S")
+            if s == 10:
+                tok_weave(0, 3, "S")
+            if s in (5, 7):
+                act_quant((s - 5) // 2)
+            if s in (9, 11):
+                tok_quant(0, (s - 9) // 2)
+
+        late = {}
+
+        def late_passes(names, steps):
+            for s in steps:
+                for x in names:
+                    if x not in late:
+                        late[x] = bank(("z2", "z0", "z1", "t0")[x])
+                    dhid_pass(late[x], s, *groups[x])
+
+        e_turn(11)
+        e_unturn(11)
+        for s in range(12, STEPS):
+            c = s - 12
+            for n in (2 * s, 2 * s + 1):
+                subtract(n)
+                if n + Z_BANKS < 2 * STEPS:
+                    z_mm(n + Z_BANKS)
+            if c == 0:
+                voc_quant(10)
+                dhid_step(10)
+            else:
+                if c == 3:
+                    voc_quant(13)
+                tok_quant(1, c - 1)
+                e_turn(s - 1)
+                e_unturn(s - 1)
+            multiply(s)
+            if c == 0:
+                voc_quant(11)
+                dhid_step(11)
+            elif c == 2:
+                voc_quant(12)
+            else:
+                tok_quant(0, 2 + c // 2)
+            if c < 3:
+                tok_weave(1, c, "V", 0, TOK_ON_VECTOR)
+                tok_weave(1, c, "S", TOK_ON_VECTOR, C)
+            else:
+                tok_weave(1, c, "V")
+                late_passes((1, 2), (12,))
+                late_passes((0, 1, 2), (13,))
+            if c == 0:
+                dhid_outs(2, "SSSS")
+                continue
+            for r in range(4):
+                dup("d%d" % r, r, c - 1)
+                if c == 3 and r == 1:
+                    e_turn(15)
+                if c == 3 and r == 2:
+                    e_unturn(15)
+                dup_out("S", r, c - 1)
+            if c == 2:
+                late_passes((0,), (12,))
+
+        voc_quant(14)
+        tok_quant(1, 3)
+        voc_quant(15)
+        late_passes((0,), (14,))
+        for x in range(4):
+            dup("d%d" % x, x, 3)
+            dup_out("S", x, 3)
+            late_passes((x,), ((15,), (14, 15), (14, 15), range(12, 16))[x])
+            dhid_out("V", late[x], 3, *groups[x])

@@ -21,8 +21,9 @@ FLOPS = 2 * M * D * V * 2 + 2 * M * R * V
 STEPS = 16
 Z_BANKS = 3
 TOK_ON_VECTOR = 256
-ON_GPSIMD = 128
+ON_GPSIMD = (0, 352, 352, 160)
 RUN = 8
+LAST_ON_VECTOR = 256
 
 
 def tile_reverse_kl_backward_s8_kernel(
@@ -39,7 +40,8 @@ def tile_reverse_kl_backward_s8_kernel(
         cen = keep.tile([P, 8], BF16, name="cen")
         cen32 = keep.tile([P, 8], F32, name="cen32")
         ident = keep.tile([P, P], F32, name="ident")
-        u_codes = keep.tile([P, 4, 2 * D], U8, name="u_codes", align_bytes=64)
+        ident16 = keep.tile([P, P], BF16, name="ident16")
+        u_codes = [keep.tile([P, 2 * D], U8, name="u_codes_%d" % c, align_bytes=64) for c in range(4)]
         u_sc = keep.tile([P, 4, D], U8, name="u_sc", align_bytes=64)
 
         def mx_tiles(pool, name, width, bufs):
@@ -59,7 +61,8 @@ def tile_reverse_kl_backward_s8_kernel(
         nc.scalar.dma_start(out=cen[:].rearrange("p (g t) -> p g t", t=4), in_=centre.rearrange("(g p t) -> p g t", p=P, t=4))
         nc.scalar.activation(out=cen32[:], in_=cen[:], func=ACT.Copy)
         make_identity(nc, ident[:])
-        nc.gpsimd.memset(u_sc[:].rearrange("p g n -> p (g n)").bitcast(I32), 0)
+        nc.gpsimd.tensor_copy(out=ident16[:], in_=ident[:])
+        nc.vector.memset(u_sc[:].rearrange("p g n -> p (g n)").bitcast(I32), 0)
 
         w_view = w_bytes.rearrange("(g p t) v -> g p t v", p=P, t=4)
         w_raw = {}
@@ -86,8 +89,16 @@ def tile_reverse_kl_backward_s8_kernel(
             act_rows[g] = work.tile([P, 4 * R], BF16, name="rows", bufs=4)
             nc.sync.dma_start(out=act_rows[g][:], in_=act[g * C : (g + 1) * C, :].rearrange("(p t) r -> p (t r)", t=4))
 
-        te = {(g, c): keep.tile([P, 4 * C], BF16, name="te_%d_%d" % (g, c)) for g in range(2) for c in range(4)}
-        pr = {(g, c): keep.tile([P, 4 * C], BF16, name="pr_%d_%d" % (g, c)) for g in range(2) for c in range(4)}
+        tp = {(g, c): keep.tile([P, 8 * C], BF16, name="tp_%d_%d" % (g, c)) for g in range(2) for c in range(4)}
+        te = {key: tile[:, : 4 * C] for key, tile in tp.items()}
+        pr = {key: tile[:, 4 * C :] for key, tile in tp.items()}
+
+        def load_tp4(c):
+            for dst, src in ((te, teach), (pr, probs)):
+                nc.sync.dma_start(
+                    out=dst[1, c].rearrange("p (t v) -> p t v", t=4),
+                    in_=src[C:, c * C : (c + 1) * C].rearrange("(p t) v -> p t v", t=4),
+                )
 
         def load_tp(s):
             j, c = divmod(s, 4)
@@ -98,46 +109,55 @@ def tile_reverse_kl_backward_s8_kernel(
                     in_=slots(src, j)[:, :, c * C : (c + 1) * C],
                 )
 
+        def load_u(c):
+            nc.sync.dma_start(out=u_codes[c][:], in_=u_words[c])
+
         load_w(0, 0, 1)
         load_w(1, 0, 1)
-        load_hid(0)
         load_w(0, 1, 1)
+        load_hid(0)
         load_w(1, 1, 1)
         load_tp(0)
-        load_hid(1)
         load_w(0, 2, 2)
         load_w(1, 2, 2)
-        load_hid(3)
+        load_hid(1)
         load_tp(1)
         load_hid(2)
+        load_hid(3)
         for q in range(4):
             nc.sync.dma_start(
                 out=u_sc[32 * q : 32 * q + 4, :, :].bitcast(I32),
                 in_=u_scales[:, 4 * q : 4 * q + 4, :].rearrange("g q n -> q g n").bitcast(I32),
             )
-        nc.sync.dma_start(out=u_codes[:], in_=u_words.rearrange("g p b -> p g b"))
+        load_u(0)
         load_tp(2)
+        load_u(1)
         load_tp(3)
         load_act(0)
+        load_u(2)
         load_tp(4)
         load_act(1)
-        for s in range(5, STEPS):
-            load_tp(s)
+        load_u(3)
+        load_tp(5)
+        load_tp(6)
+        load_tp(7)
+        for c in range(4):
+            load_tp4(c)
 
         wide = {}
 
-        def widen(kg, c, engines):
+        def widen(kg, c, engines, a=0, b=C):
             if (kg, c) not in wide:
                 wide[kg, c] = work.tile([P, 4, C], BF16, name="wide", bufs=4)
             for t in range(4):
                 if engines[t] == "-":
                     continue
-                src = w_raw[kg, c][:, t, :].bitcast(FP8)
+                src = w_raw[kg, c][:, t, a:b].bitcast(FP8)
                 sc = wsc[:, 4 * kg + t : 4 * kg + t + 1]
                 if engines[t] == "S":
-                    nc.scalar.activation(out=wide[kg, c][:, t, :], in_=src, func=ACT.Copy, scale=sc)
+                    nc.scalar.activation(out=wide[kg, c][:, t, a:b], in_=src, func=ACT.Copy, scale=sc)
                 else:
-                    nc.vector.tensor_scalar(out=wide[kg, c][:, t, :], in0=src, scalar1=sc, scalar2=None, op0=ALU.mult)
+                    nc.vector.tensor_scalar(out=wide[kg, c][:, t, a:b], in0=src, scalar1=sc, scalar2=None, op0=ALU.mult)
 
         def interleave(dst, src, engine, a, b):
             o = dst[:, 4 * a : 4 * b].rearrange("p (c i t) -> p c t i", i=RUN, t=4)
@@ -193,8 +213,8 @@ def tile_reverse_kl_backward_s8_kernel(
             turn(b, [words[:, t * C + kg * 2 * P + u : t * C + (kg + 1) * 2 * P : 2] for t in range(2) for u in range(2)])
 
         def hid_unturn(j, kg):
-            if kg == 0:
-                hid_t[j] = work.tile([P, 4 * C], BF16, name="hid_t", align_bytes=64, bufs=2)
+            if j not in hid_t:
+                hid_t[j] = work.tile([P, 4 * C], BF16, name="hid_t", align_bytes=64, bufs=3)
             unturn(hid_t[j][:, kg * 2 * C : (kg + 1) * 2 * C], turned["hid", j, kg])
 
         def hid_quant(j):
@@ -210,10 +230,11 @@ def tile_reverse_kl_backward_s8_kernel(
         def z_bank(n):
             return "z%d" % (n % Z_BANKS if n >= 6 else n % 2)
 
-        def z_mm(n):
+        def z_mm(n, halves=(0, 1)):
             j, i, g, t, c = where(n)
-            zb[n] = bank(z_bank(n))
-            for kg in range(2):
+            if n not in zb:
+                zb[n] = bank(z_bank(n))
+            for kg in halves:
                 cols = slice((2 * kg + i) * P, (2 * kg + i + 1) * P)
                 nc.tensor.matmul_mx(
                     out=zb[n][:],
@@ -240,32 +261,93 @@ def tile_reverse_kl_backward_s8_kernel(
                 op1=ALU.subtract,
             )
 
-        def multiply(s, a=0, b=2):
+        def e_block(g, c, t, u):
+            if t % 2 == 1 and u == 1:
+                return pr[g, c][:, (t - 1) * C + 2 * P : t * C]
+            return te[g, c][:, t * C + u * 2 * P : t * C + (u + 1) * 2 * P]
+
+        probs_bank = {}
+
+        def probs_to_psum(s, name):
             j, i, g, t, c = where(2 * s)
-            cols = slice(t * C, (t + 2) * C)
-            nc.vector.tensor_tensor(
-                out=te[g, c][:, cols].rearrange("p (t u x) -> p u t x", u=2, t=2)[:, a:b],
-                in0=diff[s][:].rearrange("p (x u e) -> p u x e", u=2, e=2)[:, a:b],
-                in1=pr[g, c][:, cols].rearrange("p (x u e) -> p u x e", u=2, e=2)[:, a:b],
-                op=ALU.mult,
-            )
+            probs_bank[s] = b = psum.tile([P, 2 * C], BF16, name=name)
+            for i in range(2):
+                nc.tensor.matmul(
+                    out=b[:, i * C : (i + 1) * C],
+                    lhsT=ident16[:],
+                    rhs=pr[g, c][:, (t + i) * C : (t + i + 1) * C],
+                    start=True,
+                    stop=True,
+                )
+
+        def factors(s):
+            j, i, g, t, c = where(2 * s)
+            p = probs_bank[s][:] if s in probs_bank else pr[g, c][:, t * C : (t + 2) * C]
+            view = "p (i x u e) -> p i u x e"
+            return diff[s][:].rearrange(view, i=2, u=2, e=2), p.rearrange(view, i=2, u=2, e=2), g, c, t
+
+        def multiply_first(s):
+            d, p, g, c, t = factors(s)
+            nc.vector.tensor_tensor(out=te[g, c][:, t * C : (t + 1) * C], in0=d[:, 0], in1=p[:, 0], op=ALU.mult)
+
+        def multiply_second(s):
+            d, p, g, c, t = factors(s)
+            blocks = tp[g, c][:].rearrange("p (b x) -> p b x", x=2 * P)
+            nc.vector.tensor_tensor(out=blocks[:, 2 * t + 2 : 2 * t + 10 : 7], in0=d[:, 1], in1=p[:, 1], op=ALU.mult)
+
+        def multiply_words(s):
+            d, p, g, c, t = factors(s)
+            e = te[g, c][:, t * C : (t + 2) * C].rearrange("p (i u x) -> p u i x", i=2, u=2)
+            nc.vector.tensor_tensor(out=e[:, 1, 0], in0=d[:, 0, 1], in1=p[:, 0, 1], op=ALU.mult)
+            nc.vector.tensor_tensor(out=e[:, 0], in0=d[:, :, 0], in1=p[:, :, 0], op=ALU.mult)
+
+        def multiply_last(s, engine):
+            d, p, g, c, t = factors(s)
+            engine.tensor_tensor(out=e_block(g, c, t + 1, 1), in0=d[:, 1, 1], in1=p[:, 1, 1], op=ALU.mult)
+
+        def multiply_block(s, u):
+            d, p, g, c, t = factors(s)
+            nc.vector.tensor_tensor(out=e_block(g, c, t + 1, u), in0=d[:, 1, u], in1=p[:, 1, u], op=ALU.mult)
+
+        def multiply_shared(s):
+            d, p, g, c, t = factors(s)
+            multiply_first(s)
+            nc.vector.tensor_tensor(out=e_block(g, c, t + 1, 0), in0=d[:, 1, 0], in1=p[:, 1, 0], op=ALU.mult)
+            nc.gpsimd.tensor_tensor(out=e_block(g, c, t + 1, 1), in0=d[:, 1, 1], in1=p[:, 1, 1], op=ALU.mult)
 
         e_t = {}
         voc_mx = {}
 
         def e_turn(s):
             j, i, g, t, c = where(2 * s)
-            words = te[g, c][:].bitcast(F32)
             turned["e", s] = b = bank("t0")
-            turn(b, [words[:, (2 * t + x) * P : (2 * t + x + 1) * P] for x in range(4)])
+            turn(b, [e_block(g, c, t + i, u).bitcast(F32) for i in range(2) for u in range(2)])
 
         def e_unturn(s):
             e_t[s] = work.tile([P, 2 * C], BF16, name="e_t", align_bytes=64, bufs=3)
             unturn(e_t[s][:], turned["e", s])
 
         def voc_quant(s):
-            voc_mx[s] = mx_tiles(work, "voc", 2 * P, 6)
+            voc_mx[s] = mx_tiles(work, "voc", 2 * P, 5)
             quantise(voc_mx[s], e_t[s], 0, 2 * P)
+
+        def slot_turn(s, i):
+            j, i0, g, t, c = where(2 * s)
+            turned["slot", i] = b = bank("t0")
+            turn(b, [e_block(g, c, t + i, u).bitcast(F32) for u in range(2)])
+
+        def slot_unturn(s, i):
+            if i == 0:
+                e_t[s] = work.tile([P, 2 * C], BF16, name="e_t", align_bytes=64, bufs=3)
+            nc.scalar.copy(
+                out=e_t[s][:, i * C : (i + 1) * C].bitcast(F32).rearrange("q (p u) -> q p u", u=2),
+                in_=turned["slot", i][:, : 2 * P].rearrange("q (u p) -> q p u", u=2),
+            )
+
+        def slot_quant(s, i):
+            if i == 0:
+                voc_mx[s] = mx_tiles(work, "voc", 2 * P, 5)
+            quantise(voc_mx[s], e_t[s], i * P, (i + 1) * P)
 
         def dhid_pass(b, s, i, nh):
             c = s % 4
@@ -273,14 +355,17 @@ def tile_reverse_kl_backward_s8_kernel(
                 out=b[:],
                 lhsT=voc_mx[s][0][:, i * P : (i + 1) * P].bitcast(FP8X4),
                 lhsT_scale=voc_mx[s][1][:, i * P : (i + 1) * P],
-                rhs=u_codes[:, c, nh * 2 * C : (nh + 1) * 2 * C].bitcast(FP4X4),
+                rhs=u_codes[c][:, nh * 2 * C : (nh + 1) * 2 * C].bitcast(FP4X4),
                 rhs_scale=u_sc[:, c, nh * C : (nh + 1) * C],
                 start=c == 0,
                 stop=c == 3,
             )
 
         def copy_out(engine, src, dst, shape):
-            r = work.tile([P, C], F32, name="res", bufs=6)
+            if engine == "S":
+                r = work.tile([P, C], F32, name="res", bufs=6)
+            else:
+                r = work.tile([P, C], F32, name="rows", bufs=4)
             if engine == "S":
                 nc.scalar.copy(out=shape(r[:]), in_=src)
             else:
@@ -307,10 +392,21 @@ def tile_reverse_kl_backward_s8_kernel(
         tok_mx = {}
 
         def tok_weave(g, c, engine, a=0, b=C):
-            weave(("tok", g, c), te[g, c][:].rearrange("p (t v) -> p t v", t=4), engine, a, b)
+            key = ("tok", g, c)
+            if a < 2 * P:
+                weave(key, te[g, c].rearrange("p (t v) -> p t v", t=4), engine, a, min(b, 2 * P))
+            if b > 2 * P:
+                a = max(a, 2 * P)
+                src = tp[g, c][:].rearrange("p (e h o v) -> p h e o v", e=2, h=2, o=2)[:, :, :, 0, a:b]
+                o = woven[key][:, 4 * a : 4 * b].rearrange("p (c i h e) -> p c h e i", i=RUN, h=2, e=2)
+                src = src.rearrange("p h e (c i) -> p c h e i", i=RUN)
+                if engine == "V":
+                    nc.vector.tensor_copy(out=o, in_=src)
+                else:
+                    nc.scalar.copy(out=o, in_=src)
 
         def tok_quant(g, c):
-            tok_mx[g, c] = mx_tiles(work, "tok", C, 6)
+            tok_mx[g, c] = mx_tiles(work, "tok", C, 5)
             quantise(tok_mx[g, c], woven["tok", g, c], 0, C)
 
         def act_weave(g, engine, a=0, b=R):
@@ -344,103 +440,130 @@ def tile_reverse_kl_backward_s8_kernel(
 
         hid_turn(0, 0, "d0")
         hid_turn(0, 1, "d1")
-        widen(0, 0, "VVVV")
+        widen(0, 0, "VVVS")
         widen(1, 0, "VVSS")
         w_weave(0, 0)
         w_weave(1, 0)
-        widen(0, 1, "S---")
+        widen(0, 1, "SSSS")
         hid_unturn(0, 0)
         hid_unturn(0, 1)
         w_quant(0, 0)
         w_quant(1, 0)
-        widen(0, 1, "-SSS")
         hid_quant(0)
         z_mm(0)
         z_mm(1)
+        probs_to_psum(0, "z2")
         hid_turn(1, 0, "d2")
         hid_turn(1, 1, "d3")
-        widen(1, 1, "VVSS")
         w_weave(0, 1)
-        w_weave(1, 1, "G", 0, ON_GPSIMD)
+        for c in range(1, 4):
+            if c > 1:
+                widen(0, c, "SSSS")
+            if c == 3:
+                break
+            widen(1, c, "SSS-")
+            widen(1, c, "---S", ON_GPSIMD[c], C)
 
-        widen(0, 2, "SSSS")
-        hid_unturn(1, 0)
-        hid_unturn(1, 1)
-        widen(1, 2, "SSS-")
+        def gate(c):
+            widen(1, c, "---V", 0, ON_GPSIMD[c])
+            w_weave(1, c, "G", 0, ON_GPSIMD[c])
+            w_quant(0, c)
+
+        gate(1)
+
         for s in range(3):
             c = s + 1
             subtract(2 * s)
             subtract(2 * s + 1)
+            z_mm(2 * c, (0,))
+            z_mm(2 * c + 1, (0,))
             if c < 3:
-                w_weave(1, c, "V", ON_GPSIMD, C)
-            w_quant(0, c)
-            w_quant(1, c)
-            multiply(s)
-            z_mm(2 * c)
-            z_mm(2 * c + 1)
-            if s == 2:
-                hid_turn(2, 1, "t0")
-                hid_unturn(2, 1)
-                voc_quant(1)
-                dhid_step(0, 2, 4)
-                dhid_step(1)
-            e_turn(s)
+                multiply_first(s)
+                multiply_second(s)
+                w_weave(1, c, "V", ON_GPSIMD[c], C)
+                if s == 0:
+                    w_weave(0, 2)
+                else:
+                    w_weave(0, 3, "V", 0, C // 2)
+                w_quant(1, c)
+                if s == 1:
+                    hid_turn(3, 0, "z2")
+                e_turn(s)
+                if s == 0:
+                    probs_to_psum(1, "z2")
+                z_mm(2 * c, (1,))
+                z_mm(2 * c + 1, (1,))
+            else:
+                w_quant(1, c)
+                multiply_shared(s)
+                z_mm(2 * c, (1,))
+                z_mm(2 * c + 1, (1,))
             if s == 0:
-                widen(0, 3, "SSSS")
                 e_unturn(0)
-                for kg in range(2):
-                    hid_turn(3, kg, "d%d" % (2 + kg))
                 widen(1, 3, "SSS-")
-                w_weave(0, 3, "S")
-                hid_quant(1)
-                widen(1, 2, "---V")
-                w_weave(0, 2)
-                w_weave(1, 2, "G", 0, ON_GPSIMD)
+                widen(1, 3, "---S", ON_GPSIMD[3], C)
+                hid_turn(2, 0, "d0")
+                hid_turn(2, 1, "d1")
+                hid_turn(3, 1, "t0")
+                gate(2)
+                hid_unturn(3, 1)
+                hid_unturn(1, 0)
+                hid_unturn(1, 1)
             if s == 1:
-                widen(1, 3, "---V")
-                voc_quant(0)
-                hid_turn(2, 0, "z2")
-                dhid_step(0, 0, 2)
-                w_weave(1, 3, "G", 0, ON_GPSIMD)
-                w_weave(1, 3, "S", ON_GPSIMD, C)
                 e_unturn(1)
-                for kg in range(2):
-                    hid_unturn(3, kg)
                 hid_unturn(2, 0)
-            if s == 2:
-                act_weave(0, "S")
-                e_unturn(2)
+                hid_unturn(2, 1)
+                voc_quant(0)
+                w_weave(0, 3, "V", C // 2, C)
+                hid_quant(1)
+                voc_quant(1)
+                for x in (2, 0):
+                    dhid_step(0, x, x + 2)
+                    dhid_step(1, x, x + 2)
+                gate(3)
+                w_weave(1, 3, "S", ON_GPSIMD[3], C)
+                hid_unturn(3, 0)
+        act_weave(0, "S")
+        act_weave(1, "S", 0, R // 2)
         z_mm(8)
+
+        def extras(s):
+            if s in (5, 7):
+                hid_quant((s - 1) // 2)
+            if s in (6, 8):
+                act_quant((s - 6) // 2)
+            if s >= 9:
+                tok_quant(0, s - 9)
 
         for s in range(3, 12):
             j, c = divmod(s, 4)
             for n in (2 * s, 2 * s + 1):
                 subtract(n)
                 z_mm(n + Z_BANKS)
-            if s > 3:
-                e_turn(s - 1)
-                e_unturn(s - 1)
-            if s > 3:
+            e_turn(s - 1)
+            e_unturn(s - 1)
+            if s == 3:
+                multiply_shared(s)
+            elif s < 11:
+                extras(s)
+                multiply_words(s)
+                multiply_last(s, nc.gpsimd)
                 voc_quant(s - 2)
             else:
-                hid_quant(3)
-            multiply(s)
-            if s == 3:
-                hid_quant(2)
+                extras(s)
+                multiply_first(s)
+                voc_quant(s - 2)
+                multiply_second(s)
             if s > 3:
                 dhid_step(s - 2)
                 if s % 4 == 1:
                     dhid_outs(s // 4 - 1, "SSSS")
             if s == 3:
-                act_weave(1, "S")
+                act_weave(1, "S", R // 2, R)
             if s in (6, 7, 8):
                 tok_weave(0, s - 6, "S")
             if s == 10:
                 tok_weave(0, 3, "S")
-            if s in (5, 7):
-                act_quant((s - 5) // 2)
-            if s in (9, 11):
-                tok_quant(0, (s - 9) // 2)
 
         late = {}
 
@@ -448,60 +571,90 @@ def tile_reverse_kl_backward_s8_kernel(
             for s in steps:
                 for x in names:
                     if x not in late:
-                        late[x] = bank(("z2", "z0", "z1", "t0")[x])
+                        late[x] = bank(("z2", "z0", "z1", "d0")[x])
                     dhid_pass(late[x], s, *groups[x])
+
+        def dups(c, rows, names=("d0", "d1", "d2", "d3")):
+            for r in rows:
+                dup(names[r], r, c)
+
+        def dup_outs(c, rows):
+            for r in rows:
+                dup_out("S", r, c)
 
         e_turn(11)
         e_unturn(11)
-        for s in range(12, STEPS):
-            c = s - 12
-            for n in (2 * s, 2 * s + 1):
-                subtract(n)
-                if n + Z_BANKS < 2 * STEPS:
-                    z_mm(n + Z_BANKS)
-            if c == 0:
-                voc_quant(10)
-                dhid_step(10)
-            else:
-                if c == 3:
-                    voc_quant(13)
-                tok_quant(1, c - 1)
-                e_turn(s - 1)
-                e_unturn(s - 1)
-            multiply(s)
-            if c == 0:
-                voc_quant(11)
-                dhid_step(11)
-            elif c == 2:
-                voc_quant(12)
-            else:
-                tok_quant(0, 2 + c // 2)
-            if c < 3:
-                tok_weave(1, c, "V", 0, TOK_ON_VECTOR)
-                tok_weave(1, c, "S", TOK_ON_VECTOR, C)
-            else:
-                tok_weave(1, c, "V")
-                late_passes((1, 2), (12,))
-                late_passes((0, 1, 2), (13,))
-            if c == 0:
-                dhid_outs(2, "SSSS")
-                continue
-            for r in range(4):
-                dup("d%d" % r, r, c - 1)
-                if c == 3 and r == 1:
-                    e_turn(15)
-                if c == 3 and r == 2:
-                    e_unturn(15)
-                dup_out("S", r, c - 1)
-            if c == 2:
-                late_passes((0,), (12,))
+        subtract(24)
+        subtract(25)
+        z_mm(27)
+        z_mm(28)
+        voc_quant(10)
+        dhid_step(10)
+        multiply_words(12)
+        voc_quant(11)
+        dhid_step(11)
+        multiply_last(12, nc.vector)
+        tok_weave(1, 0, "V", 0, 2 * P)
+        tok_weave(1, 0, "S", 2 * P, C)
 
+        subtract(26)
+        subtract(27)
+        tok_quant(1, 0)
+        e_turn(12)
+        z_mm(29)
+        z_mm(30)
+        dhid_outs(2, "SSSS")
+        e_unturn(12)
+        dups(0, range(4))
+        multiply_words(13)
+        tok_quant(0, 3)
+        multiply_last(13, nc.vector)
+        tok_weave(1, 1, "V", 0, 2 * P)
+        tok_weave(1, 1, "S", 2 * P, C)
+        dup_outs(0, range(4))
+
+        subtract(28)
+        subtract(29)
+        tok_quant(1, 1)
+        z_mm(31)
+        e_turn(13)
+        e_unturn(13)
+        dups(1, range(4))
+        dup_outs(1, range(4))
+        multiply_words(14)
+        voc_quant(12)
+        multiply_last(14, nc.vector)
+        late_passes((0,), (12,))
+        e_turn(14)
+        e_unturn(14)
+        tok_weave(1, 2, "V")
+        voc_quant(13)
+        tok_quant(1, 2)
+        late_passes((0,), (13,))
+
+        subtract(30)
+        subtract(31)
+        dups(2, range(4))
+        dup_outs(2, range(2))
+        multiply_words(15)
         voc_quant(14)
-        tok_quant(1, 3)
-        voc_quant(15)
+        multiply_last(15, nc.vector)
+        e_turn(15)
+        e_unturn(15)
+        dup_outs(2, range(2, 4))
         late_passes((0,), (14,))
-        for x in range(4):
-            dup("d%d" % x, x, 3)
-            dup_out("S", x, 3)
-            late_passes((x,), ((15,), (14, 15), (14, 15), range(12, 16))[x])
-            dhid_out("V", late[x], 3, *groups[x])
+        late_passes((1,), (12, 13, 14))
+        late_passes((2,), (12,))
+        tok_weave(1, 3, "V")
+        voc_quant(15)
+        tok_quant(1, 3)
+        late_passes((0, 1), (15,))
+        dhid_out("S", late[0], 3, *groups[0])
+        dhid_out("V", late[1], 3, *groups[1])
+        for r in range(4):
+            dup(("d1", "d2", "d3", "t0")[r], r, 3)
+            dup_out("SV"[r % 2], r, 3)
+        late_passes((2,), (13, 14, 15))
+        dhid_out("S", late[2], 3, *groups[2])
+        late_passes((3,), range(12, 16))
+        dhid_out("V", late[3], 3, *groups[3])

@@ -301,6 +301,14 @@ def tile_reverse_kl_backward_s8_kernel(
             nc.vector.tensor_tensor(out=e[:, 1, 0], in0=d[:, 0, 1], in1=p[:, 0, 1], op=ALU.mult)
             nc.vector.tensor_tensor(out=e[:, 0], in0=d[:, :, 0], in1=p[:, :, 0], op=ALU.mult)
 
+        def multiply_part(s, part):
+            d, p, g, c, t = factors(s)
+            e = te[g, c][:, t * C : (t + 2) * C].rearrange("p (i u x) -> p u i x", i=2, u=2)
+            if part == 0:
+                nc.vector.tensor_tensor(out=e[:, 1, 0], in0=d[:, 0, 1], in1=p[:, 0, 1], op=ALU.mult)
+            else:
+                nc.vector.tensor_tensor(out=e[:, 0], in0=d[:, :, 0], in1=p[:, :, 0], op=ALU.mult)
+
         def multiply_last(s, engine):
             d, p, g, c, t = factors(s)
             engine.tensor_tensor(out=e_block(g, c, t + 1, 1), in0=d[:, 1, 1], in1=p[:, 1, 1], op=ALU.mult)
@@ -318,9 +326,9 @@ def tile_reverse_kl_backward_s8_kernel(
         e_t = {}
         voc_mx = {}
 
-        def e_turn(s):
+        def e_turn(s, name="t0"):
             j, i, g, t, c = where(2 * s)
-            turned["e", s] = b = bank("t0")
+            turned["e", s] = b = bank(name)
             turn(b, [e_block(g, c, t + i, u).bitcast(F32) for i in range(2) for u in range(2)])
 
         def e_unturn(s):
@@ -361,9 +369,32 @@ def tile_reverse_kl_backward_s8_kernel(
                 stop=c == 3,
             )
 
+        def half_pass(b, s, half):
+            c = s % 4
+            a = C + half * 2 * P
+            nc.tensor.matmul_mx(
+                out=b[:, : 2 * P],
+                lhsT=voc_mx[s][0][:, P:].bitcast(FP8X4),
+                lhsT_scale=voc_mx[s][1][:, P:],
+                rhs=u_codes[c][:, 2 * a : 2 * (a + 2 * P)].bitcast(FP4X4),
+                rhs_scale=u_sc[:, c, a : a + 2 * P],
+                start=c == 0,
+                stop=c == 3,
+            )
+
+        def half_out(engine, b, half):
+            a = C + half * 2 * P
+            if engine == "S":
+                r = work.tile([P, 2 * P], F32, name="res", bufs=5)
+                nc.scalar.copy(out=r[:], in_=b[:, : 2 * P])
+            else:
+                r = work.tile([P, 2 * P], F32, name="rows", bufs=4)
+                nc.vector.tensor_copy(out=r[:], in_=b[:, : 2 * P])
+            nc.sync.dma_start(out=slots(out_0, 3)[:, 1, a : a + 2 * P], in_=r[:])
+
         def copy_out(engine, src, dst, shape):
             if engine == "S":
-                r = work.tile([P, C], F32, name="res", bufs=6)
+                r = work.tile([P, C], F32, name="res", bufs=5)
             else:
                 r = work.tile([P, C], F32, name="rows", bufs=4)
             if engine == "S":
@@ -406,7 +437,7 @@ def tile_reverse_kl_backward_s8_kernel(
                     nc.scalar.copy(out=o, in_=src)
 
         def tok_quant(g, c):
-            tok_mx[g, c] = mx_tiles(work, "tok", C, 5)
+            tok_mx[g, c] = mx_tiles(work, "tok", C, 6)
             quantise(tok_mx[g, c], woven["tok", g, c], 0, C)
 
         def act_weave(g, engine, a=0, b=R):
@@ -449,6 +480,7 @@ def tile_reverse_kl_backward_s8_kernel(
         hid_unturn(0, 1)
         w_quant(0, 0)
         w_quant(1, 0)
+        widen(1, 1, "V---")
         hid_quant(0)
         z_mm(0)
         z_mm(1)
@@ -461,7 +493,7 @@ def tile_reverse_kl_backward_s8_kernel(
                 widen(0, c, "SSSS")
             if c == 3:
                 break
-            widen(1, c, "SSS-")
+            widen(1, c, "-SS-" if c == 1 else "SSS-")
             widen(1, c, "---S", ON_GPSIMD[c], C)
 
         def gate(c):
@@ -528,42 +560,45 @@ def tile_reverse_kl_backward_s8_kernel(
         z_mm(8)
 
         def extras(s):
-            if s in (5, 7):
-                hid_quant((s - 1) // 2)
-            if s in (6, 8):
-                act_quant((s - 6) // 2)
-            if s >= 9:
-                tok_quant(0, s - 9)
+            if s == 6:
+                hid_quant(2)
+            if s == 7:
+                act_quant(0)
+            if s == 8:
+                act_quant(1)
+            if s == 9:
+                tok_quant(0, 0)
+            if s == 10:
+                hid_quant(3)
+            if s == 11:
+                tok_quant(0, 1)
 
         for s in range(3, 12):
             j, c = divmod(s, 4)
-            for n in (2 * s, 2 * s + 1):
-                subtract(n)
-                z_mm(n + Z_BANKS)
-            e_turn(s - 1)
-            e_unturn(s - 1)
+            subtract(2 * s)
+            subtract(2 * s + 1)
+            extras(s)
+            z_mm(2 * s + Z_BANKS)
             if s == 3:
+                e_turn(2)
+                e_unturn(2)
+            z_mm(2 * s + 1 + Z_BANKS)
+            if s > 3:
+                e_turn(s - 1)
+                e_unturn(s - 1)
+            if s < 4:
                 multiply_shared(s)
-            elif s < 11:
-                extras(s)
+            else:
                 multiply_words(s)
                 multiply_last(s, nc.gpsimd)
                 voc_quant(s - 2)
-            else:
-                extras(s)
-                multiply_first(s)
-                voc_quant(s - 2)
-                multiply_second(s)
-            if s > 3:
                 dhid_step(s - 2)
                 if s % 4 == 1:
                     dhid_outs(s // 4 - 1, "SSSS")
             if s == 3:
                 act_weave(1, "S", R // 2, R)
-            if s in (6, 7, 8):
-                tok_weave(0, s - 6, "S")
-            if s == 10:
-                tok_weave(0, 3, "S")
+            if s in (4, 6, 7, 8):
+                tok_weave(0, max(s - 5, 0), "S")
 
         late = {}
 
@@ -582,69 +617,71 @@ def tile_reverse_kl_backward_s8_kernel(
             for r in rows:
                 dup_out("S", r, c)
 
-        e_turn(11)
-        e_unturn(11)
         subtract(24)
         subtract(25)
+        e_turn(11)
+        e_unturn(11)
         z_mm(27)
         z_mm(28)
         voc_quant(10)
         dhid_step(10)
-        multiply_words(12)
+        multiply_part(12, 0)
+        tok_quant(0, 2)
+        multiply_part(12, 1)
+        multiply_last(12, nc.gpsimd)
         voc_quant(11)
         dhid_step(11)
-        multiply_last(12, nc.vector)
-        tok_weave(1, 0, "V", 0, 2 * P)
-        tok_weave(1, 0, "S", 2 * P, C)
+        tok_weave(1, 0, "S", 0, 2 * P)
 
         subtract(26)
         subtract(27)
+        tok_weave(1, 0, "V", 2 * P, C)
+        multiply_part(13, 0)
         tok_quant(1, 0)
-        e_turn(12)
         z_mm(29)
         z_mm(30)
         dhid_outs(2, "SSSS")
-        e_unturn(12)
         dups(0, range(4))
-        multiply_words(13)
+        multiply_part(13, 1)
+        multiply_last(13, nc.gpsimd)
         tok_quant(0, 3)
-        multiply_last(13, nc.vector)
-        tok_weave(1, 1, "V", 0, 2 * P)
-        tok_weave(1, 1, "S", 2 * P, C)
+        tok_weave(1, 1, "S", 0, 2 * P)
         dup_outs(0, range(4))
 
         subtract(28)
         subtract(29)
+        tok_weave(1, 1, "V", 2 * P, C)
+        multiply_words(14)
         tok_quant(1, 1)
         z_mm(31)
+        e_turn(12, "z2")
         e_turn(13)
+        e_unturn(12)
         e_unturn(13)
         dups(1, range(4))
         dup_outs(1, range(4))
-        multiply_words(14)
-        voc_quant(12)
         multiply_last(14, nc.vector)
-        late_passes((0,), (12,))
         e_turn(14)
         e_unturn(14)
         tok_weave(1, 2, "V")
-        voc_quant(13)
+        voc_quant(12)
         tok_quant(1, 2)
-        late_passes((0,), (13,))
+        voc_quant(13)
+        late_passes((0,), (12, 13))
 
         subtract(30)
         subtract(31)
-        dups(2, range(4))
+        dups(2, range(3))
         dup_outs(2, range(2))
         multiply_words(15)
         voc_quant(14)
         multiply_last(15, nc.vector)
         e_turn(15)
         e_unturn(15)
+        dups(2, range(3, 4))
         dup_outs(2, range(2, 4))
         late_passes((0,), (14,))
         late_passes((1,), (12, 13, 14))
-        late_passes((2,), (12,))
         tok_weave(1, 3, "V")
         voc_quant(15)
         tok_quant(1, 3)
@@ -654,7 +691,10 @@ def tile_reverse_kl_backward_s8_kernel(
         for r in range(4):
             dup(("d1", "d2", "d3", "t0")[r], r, 3)
             dup_out("SV"[r % 2], r, 3)
-        late_passes((2,), (13, 14, 15))
+        late_passes((2,), range(12, 16))
         dhid_out("S", late[2], 3, *groups[2])
-        late_passes((3,), range(12, 16))
-        dhid_out("V", late[3], 3, *groups[3])
+        for half, name, engine in ((0, "d0", "V"), (1, "z2", "S")):
+            b = bank(name)
+            for s in range(12, 16):
+                half_pass(b, s, half)
+            half_out(engine, b, half)

@@ -21,7 +21,7 @@ FLOPS = 2 * M * D * V * 2 + 2 * M * R * V
 STEPS = 16
 Z_BANKS = 3
 TOK_ON_VECTOR = 256
-ON_GPSIMD = (0, 352, 352, 160)
+ON_GPSIMD = (0, 336, 336, 128)
 RUN = 8
 LAST_ON_VECTOR = 256
 
@@ -61,7 +61,7 @@ def tile_reverse_kl_backward_s8_kernel(
         nc.scalar.dma_start(out=cen[:].rearrange("p (g t) -> p g t", t=4), in_=centre.rearrange("(g p t) -> p g t", p=P, t=4))
         nc.scalar.activation(out=cen32[:], in_=cen[:], func=ACT.Copy)
         make_identity(nc, ident[:])
-        nc.gpsimd.tensor_copy(out=ident16[:], in_=ident[:])
+        nc.scalar.copy(out=ident16[:], in_=ident[:])
         nc.vector.memset(u_sc[:].rearrange("p g n -> p (g n)").bitcast(I32), 0)
 
         w_view = w_bytes.rearrange("(g p t) v -> g p t v", p=P, t=4)
@@ -132,16 +132,16 @@ def tile_reverse_kl_backward_s8_kernel(
         load_u(0)
         load_tp(2)
         load_u(1)
-        load_tp(3)
         load_act(0)
-        load_u(2)
-        load_tp(4)
+        load_tp(3)
         load_act(1)
+        load_tp(4)
+        load_u(2)
         load_u(3)
         load_tp(5)
         load_tp(6)
         load_tp(7)
-        for c in range(4):
+        for c in range(3):
             load_tp4(c)
 
         wide = {}
@@ -180,7 +180,7 @@ def tile_reverse_kl_backward_s8_kernel(
 
         def weave(key, src, engine, a=0, b=C):
             if key not in woven:
-                woven[key] = work.tile([P, 4 * C], BF16, name="woven", align_bytes=64, bufs=5)
+                woven[key] = work.tile([P, 4 * C], BF16, name="woven", align_bytes=64, bufs=4)
             interleave(woven[key], src, engine, a, b)
 
         w_mx = {(kg, c): mx_tiles(keep, "w_%d_%d" % (kg, c), C, 1) for kg in range(2) for c in range(4)}
@@ -251,7 +251,7 @@ def tile_reverse_kl_backward_s8_kernel(
         def subtract(n):
             j, i, g, t, c = where(n)
             if i == 0:
-                diff[n // 2] = work.tile([P, 2 * C], F32, name="diff", bufs=2)
+                diff[n // 2] = work.tile([P, 2 * C], F32, name="diff", bufs=3)
             nc.vector.scalar_tensor_tensor(
                 out=diff[n // 2][:, i * C : (i + 1) * C],
                 in0=zb[n][:],
@@ -332,11 +332,11 @@ def tile_reverse_kl_backward_s8_kernel(
             turn(b, [e_block(g, c, t + i, u).bitcast(F32) for i in range(2) for u in range(2)])
 
         def e_unturn(s):
-            e_t[s] = work.tile([P, 2 * C], BF16, name="e_t", align_bytes=64, bufs=3)
+            e_t[s] = work.tile([P, 2 * C], BF16, name="e_t", align_bytes=64, bufs=2)
             unturn(e_t[s][:], turned["e", s])
 
         def voc_quant(s):
-            voc_mx[s] = mx_tiles(work, "voc", 2 * P, 5)
+            voc_mx[s] = mx_tiles(work, "voc", 2 * P, 4)
             quantise(voc_mx[s], e_t[s], 0, 2 * P)
 
         def slot_turn(s, i):
@@ -346,7 +346,7 @@ def tile_reverse_kl_backward_s8_kernel(
 
         def slot_unturn(s, i):
             if i == 0:
-                e_t[s] = work.tile([P, 2 * C], BF16, name="e_t", align_bytes=64, bufs=3)
+                e_t[s] = work.tile([P, 2 * C], BF16, name="e_t", align_bytes=64, bufs=2)
             nc.scalar.copy(
                 out=e_t[s][:, i * C : (i + 1) * C].bitcast(F32).rearrange("q (p u) -> q p u", u=2),
                 in_=turned["slot", i][:, : 2 * P].rearrange("q (u p) -> q p u", u=2),
@@ -354,7 +354,7 @@ def tile_reverse_kl_backward_s8_kernel(
 
         def slot_quant(s, i):
             if i == 0:
-                voc_mx[s] = mx_tiles(work, "voc", 2 * P, 5)
+                voc_mx[s] = mx_tiles(work, "voc", 2 * P, 4)
             quantise(voc_mx[s], e_t[s], i * P, (i + 1) * P)
 
         def dhid_pass(b, s, i, nh):
@@ -385,7 +385,7 @@ def tile_reverse_kl_backward_s8_kernel(
         def half_out(engine, b, half):
             a = C + half * 2 * P
             if engine == "S":
-                r = work.tile([P, 2 * P], F32, name="res", bufs=5)
+                r = work.tile([P, 2 * P], F32, name="res", bufs=6)
                 nc.scalar.copy(out=r[:], in_=b[:, : 2 * P])
             else:
                 r = work.tile([P, 2 * P], F32, name="rows", bufs=4)
@@ -394,7 +394,7 @@ def tile_reverse_kl_backward_s8_kernel(
 
         def copy_out(engine, src, dst, shape):
             if engine == "S":
-                r = work.tile([P, C], F32, name="res", bufs=5)
+                r = work.tile([P, C], F32, name="res", bufs=6)
             else:
                 r = work.tile([P, C], F32, name="rows", bufs=4)
             if engine == "S":
@@ -595,10 +595,15 @@ def tile_reverse_kl_backward_s8_kernel(
                 dhid_step(s - 2)
                 if s % 4 == 1:
                     dhid_outs(s // 4 - 1, "SSSS")
+                if s == 5:
+                    for late_c in range(3, 4):
+                        load_tp4(late_c)
             if s == 3:
                 act_weave(1, "S", R // 2, R)
-            if s in (4, 6, 7, 8):
+            if s in (4, 6, 7):
                 tok_weave(0, max(s - 5, 0), "S")
+            if s in (8, 10):
+                tok_weave(0, 3, "S", (s - 8) * P, (s - 6) * P)
 
         late = {}
 

@@ -18,12 +18,13 @@ M, D, V, R = 1024, 1024, 2048, 512
 P = 128
 C = 512
 FLOPS = 2 * M * D * V * 2 + 2 * M * R * V
-STEPS = 16
-Z_BANKS = 3
-TOK_ON_VECTOR = 256
-ON_GPSIMD = (0, 336, 336, 128)
 RUN = 8
-LAST_ON_VECTOR = 256
+SHARE = 336
+REST = "SSVVS"
+Z3_FROM = 18
+MOVED = ((False, False, True, True), (True,) * 4)
+BLOCKS = [(0, 0, 1), (0, 1, 1), (0, 2, 2), (1, 0, 4)]
+ORDER = [(j, c) for c in range(4) for j in (0, 1)] + [(j, c) for j in (2, 3) for c in range(4)]
 
 
 def tile_reverse_kl_backward_s8_kernel(
@@ -55,15 +56,6 @@ def tile_reverse_kl_backward_s8_kernel(
         def bank(name):
             return psum.tile([P, C], F32, name=name)
 
-        nc.scalar.dma_start(
-            out=wsc[:].rearrange("p (g t) -> p g t", t=4), in_=w_scale.rearrange("(g p t) o -> p g (t o)", p=P, t=4)
-        )
-        nc.scalar.dma_start(out=cen[:].rearrange("p (g t) -> p g t", t=4), in_=centre.rearrange("(g p t) -> p g t", p=P, t=4))
-        nc.scalar.activation(out=cen32[:], in_=cen[:], func=ACT.Copy)
-        make_identity(nc, ident[:])
-        nc.scalar.copy(out=ident16[:], in_=ident[:])
-        nc.vector.memset(u_sc[:].rearrange("p g n -> p (g n)").bitcast(I32), 0)
-
         w_view = w_bytes.rearrange("(g p t) v -> g p t v", p=P, t=4)
         w_raw = {}
 
@@ -89,109 +81,78 @@ def tile_reverse_kl_backward_s8_kernel(
             act_rows[g] = work.tile([P, 4 * R], BF16, name="rows", bufs=4)
             nc.sync.dma_start(out=act_rows[g][:], in_=act[g * C : (g + 1) * C, :].rearrange("(p t) r -> p (t r)", t=4))
 
-        tp = {(g, c): keep.tile([P, 8 * C], BF16, name="tp_%d_%d" % (g, c)) for g in range(2) for c in range(4)}
-        te = {key: tile[:, : 4 * C] for key, tile in tp.items()}
-        pr = {key: tile[:, 4 * C :] for key, tile in tp.items()}
+        tp = {}
+        for g, c, n in BLOCKS:
+            tile = keep.tile([P, 8 * n * C], BF16, name="tp_%d_%d" % (g, c))
+            for i in range(n):
+                tp[g, c + i] = tile[:].rearrange("p (x t v) -> p x t v", x=2, t=4)[:, :, :, i * C : (i + 1) * C]
+            tp["block", g, c] = tile, n
 
-        def load_tp4(c):
-            for dst, src in ((te, teach), (pr, probs)):
-                nc.sync.dma_start(
-                    out=dst[1, c].rearrange("p (t v) -> p t v", t=4),
-                    in_=src[C:, c * C : (c + 1) * C].rearrange("(p t) v -> p t v", t=4),
-                )
-
-        def load_tp(s):
-            j, c = divmod(s, 4)
+        def load_tp(j, c):
             g, h = divmod(j, 2)
-            for dst, src in ((te, teach), (pr, probs)):
+            tile, n = tp["block", g, c]
+            for x, src in enumerate((teach, probs)):
+                a = (4 * x + 2 * h) * n * C
                 nc.sync.dma_start(
-                    out=dst[g, c][:, 2 * h * C : (2 * h + 2) * C].rearrange("p (t v) -> p t v", t=2),
-                    in_=slots(src, j)[:, :, c * C : (c + 1) * C],
+                    out=tile[:, a : a + 2 * n * C].rearrange("p (t v) -> p t v", t=2),
+                    in_=slots(src, j)[:, :, c * C : (c + n) * C],
                 )
 
         def load_u(c):
             nc.sync.dma_start(out=u_codes[c][:], in_=u_words[c])
 
-        load_w(0, 0, 1)
-        load_w(1, 0, 1)
-        load_w(0, 1, 1)
-        load_hid(0)
-        load_w(1, 1, 1)
-        load_tp(0)
-        load_w(0, 2, 2)
-        load_w(1, 2, 2)
-        load_hid(1)
-        load_tp(1)
-        load_hid(2)
-        load_hid(3)
-        for q in range(4):
-            nc.sync.dma_start(
-                out=u_sc[32 * q : 32 * q + 4, :, :].bitcast(I32),
-                in_=u_scales[:, 4 * q : 4 * q + 4, :].rearrange("g q n -> q g n").bitcast(I32),
-            )
-        load_u(0)
-        load_tp(2)
-        load_u(1)
-        load_act(0)
-        load_tp(3)
-        load_act(1)
-        load_tp(4)
-        load_u(2)
-        load_u(3)
-        load_tp(5)
-        load_tp(6)
-        load_tp(7)
-        for c in range(3):
-            load_tp4(c)
+        def load_u_scales():
+            for r in range(4):
+                nc.sync.dma_start(
+                    out=u_sc[r:P:32, :, :].bitcast(I32),
+                    in_=u_scales[:, r:16:4, :].rearrange("g q n -> q g n").bitcast(I32),
+                )
 
         wide = {}
+        woven = {}
 
-        def widen(kg, c, engines, a=0, b=C):
-            if (kg, c) not in wide:
-                wide[kg, c] = work.tile([P, 4, C], BF16, name="wide", bufs=4)
+        def widen(k, engines, a=0, b=C):
+            c, kg = divmod(k, 2)
+            if k not in wide:
+                wide[k] = work.tile([P, 4, C], BF16, name="wide", bufs=3)
             for t in range(4):
-                if engines[t] == "-":
-                    continue
                 src = w_raw[kg, c][:, t, a:b].bitcast(FP8)
                 sc = wsc[:, 4 * kg + t : 4 * kg + t + 1]
                 if engines[t] == "S":
-                    nc.scalar.activation(out=wide[kg, c][:, t, a:b], in_=src, func=ACT.Copy, scale=sc)
-                else:
-                    nc.vector.tensor_scalar(out=wide[kg, c][:, t, a:b], in0=src, scalar1=sc, scalar2=None, op0=ALU.mult)
+                    nc.scalar.activation(out=wide[k][:, t, a:b], in_=src, func=ACT.Copy, scale=sc)
+                elif engines[t] == "V":
+                    nc.vector.tensor_scalar(out=wide[k][:, t, a:b], in0=src, scalar1=sc, scalar2=None, op0=ALU.mult)
 
-        def interleave(dst, src, engine, a, b):
-            o = dst[:, 4 * a : 4 * b].rearrange("p (c i t) -> p c t i", i=RUN, t=4)
-            s = src[:, :, a:b].rearrange("p t (c i) -> p c t i", i=RUN)
-            if engine == "V":
-                nc.vector.tensor_copy(out=o, in_=s)
-            elif engine == "S":
-                nc.scalar.copy(out=o, in_=s)
-            else:
+        def weave(key, src, engine, a=0, b=C):
+            if key not in woven:
+                woven[key] = work.tile([P, 4 * C], BF16, name="woven", align_bytes=64, bufs=5)
+            dst = woven[key][:, 4 * a : 4 * b]
+            if engine == "G":
                 nc.gpsimd.tensor_scalar(
-                    out=dst[:, 4 * a : 4 * b].rearrange("p (c t) -> p c t", t=4),
+                    out=dst.rearrange("p (c t) -> p c t", t=4),
                     in0=src[:, :, a:b].rearrange("p t c -> p c t"),
                     scalar1=1.0,
                     scalar2=0.0,
                     op0=ALU.mult,
                     op1=ALU.add,
                 )
+                return
+            o = dst.rearrange("p (c i t) -> p c t i", i=RUN, t=4)
+            s = src[:, :, a:b].rearrange("p t (c i) -> p c t i", i=RUN)
+            if engine == "V":
+                nc.vector.tensor_copy(out=o, in_=s)
+            else:
+                nc.scalar.copy(out=o, in_=s)
 
-        woven = {}
-
-        def weave(key, src, engine, a=0, b=C):
-            if key not in woven:
-                woven[key] = work.tile([P, 4 * C], BF16, name="woven", align_bytes=64, bufs=4)
-            interleave(woven[key], src, engine, a, b)
-
-        w_mx = {(kg, c): mx_tiles(keep, "w_%d_%d" % (kg, c), C, 1) for kg in range(2) for c in range(4)}
+        w_mx = {k: mx_tiles(keep, "w_%d" % k, C, 1) for k in range(8)}
         hid_mx = {j: mx_tiles(keep, "hid_%d" % j, C, 1) for j in range(4)}
         act_mx = {g: mx_tiles(keep, "act_%d" % g, R, 1) for g in range(2)}
 
-        def w_weave(kg, c, engine="V", a=0, b=C):
-            weave(("w", kg, c), wide[kg, c][:], engine, a, b)
+        def w_weave(k, engine, a=0, b=C):
+            weave(("w", k), wide[k][:], engine, a, b)
 
-        def w_quant(kg, c):
-            quantise(w_mx[kg, c], woven["w", kg, c], 0, C)
+        def w_quant(k):
+            quantise(w_mx[k], woven["w", k], 0, C)
 
         def turn(b, words):
             for i, w in enumerate(words):
@@ -204,7 +165,6 @@ def tile_reverse_kl_backward_s8_kernel(
             )
 
         hid_t = {}
-
         turned = {}
 
         def hid_turn(j, kg, name):
@@ -214,34 +174,31 @@ def tile_reverse_kl_backward_s8_kernel(
 
         def hid_unturn(j, kg):
             if j not in hid_t:
-                hid_t[j] = work.tile([P, 4 * C], BF16, name="hid_t", align_bytes=64, bufs=3)
+                hid_t[j] = work.tile([P, 4 * C], BF16, name="hid_t", align_bytes=64, bufs=2)
             unturn(hid_t[j][:, kg * 2 * C : (kg + 1) * 2 * C], turned["hid", j, kg])
 
         def hid_quant(j):
             quantise(hid_mx[j], hid_t[j], 0, C)
 
-        def where(n):
-            s, i = divmod(n, 2)
-            j, c = divmod(s, 4)
-            return j, i, j // 2, 2 * (j % 2) + i, c
+        def where(s):
+            j, c = ORDER[s]
+            return j, c, j // 2, 2 * (j % 2)
 
         zb = {}
 
-        def z_bank(n):
-            return "z%d" % (n % Z_BANKS if n >= 6 else n % 2)
-
         def z_mm(n, halves=(0, 1)):
-            j, i, g, t, c = where(n)
+            s, i = divmod(n, 2)
+            j, c, g, t = where(s)
             if n not in zb:
-                zb[n] = bank(z_bank(n))
+                zb[n] = bank("z%d" % (n % 2 if n < Z3_FROM else n % 3))
             for kg in halves:
                 cols = slice((2 * kg + i) * P, (2 * kg + i + 1) * P)
                 nc.tensor.matmul_mx(
                     out=zb[n][:],
                     lhsT=hid_mx[j][0][:, cols].bitcast(FP8X4),
                     lhsT_scale=hid_mx[j][1][:, cols],
-                    rhs=w_mx[kg, c][0][:].bitcast(FP8X4),
-                    rhs_scale=w_mx[kg, c][1][:],
+                    rhs=w_mx[2 * c + kg][0][:].bitcast(FP8X4),
+                    rhs_scale=w_mx[2 * c + kg][1][:],
                     start=kg == 0,
                     stop=kg == 1,
                 )
@@ -249,188 +206,112 @@ def tile_reverse_kl_backward_s8_kernel(
         diff = {}
 
         def subtract(n):
-            j, i, g, t, c = where(n)
+            s, i = divmod(n, 2)
+            j, c, g, t = where(s)
             if i == 0:
-                diff[n // 2] = work.tile([P, 2 * C], F32, name="diff", bufs=3)
+                diff[s] = work.tile([P, 2 * C], F32, name="diff", bufs=2)
             nc.vector.scalar_tensor_tensor(
-                out=diff[n // 2][:, i * C : (i + 1) * C],
+                out=diff[s][:, i * C : (i + 1) * C],
                 in0=zb[n][:],
-                scalar=cen32[:, 4 * g + t : 4 * g + t + 1],
-                in1=te[g, c][:, t * C : (t + 1) * C],
+                scalar=cen32[:, 4 * g + t + i : 4 * g + t + i + 1],
+                in1=tp[g, c][:, 0, t + i, :],
                 op0=ALU.subtract,
                 op1=ALU.subtract,
             )
 
-        def e_block(g, c, t, u):
-            if t % 2 == 1 and u == 1:
-                return pr[g, c][:, (t - 1) * C + 2 * P : t * C]
-            return te[g, c][:, t * C + u * 2 * P : t * C + (u + 1) * 2 * P]
+        def e_block(s, i, u):
+            j, c, g, t = where(s)
+            if i == 1 and u == 1 and MOVED[g][c]:
+                return tp[g, c][:, 1, t, 2 * P :]
+            return tp[g, c][:, 0, t + i, u * 2 * P : (u + 1) * 2 * P]
 
         probs_bank = {}
 
-        def probs_to_psum(s, name):
-            j, i, g, t, c = where(2 * s)
-            probs_bank[s] = b = psum.tile([P, 2 * C], BF16, name=name)
+        def probs_to_psum(s):
+            j, c, g, t = where(s)
+            probs_bank[s] = b = psum.tile([P, 2 * C], BF16, name="z2")
             for i in range(2):
                 nc.tensor.matmul(
-                    out=b[:, i * C : (i + 1) * C],
-                    lhsT=ident16[:],
-                    rhs=pr[g, c][:, (t + i) * C : (t + i + 1) * C],
-                    start=True,
-                    stop=True,
+                    out=b[:, i * C : (i + 1) * C], lhsT=ident16[:], rhs=tp[g, c][:, 1, t + i, :], start=True, stop=True
                 )
 
-        def factors(s):
-            j, i, g, t, c = where(2 * s)
-            p = probs_bank[s][:] if s in probs_bank else pr[g, c][:, t * C : (t + 2) * C]
-            view = "p (i x u e) -> p i u x e"
-            return diff[s][:].rearrange(view, i=2, u=2, e=2), p.rearrange(view, i=2, u=2, e=2), g, c, t
+        def factors(s, i):
+            j, c, g, t = where(s)
+            p = probs_bank[s][:, i * C : (i + 1) * C] if s in probs_bank else tp[g, c][:, 1, t + i, :]
+            view = "p (x u e) -> p u x e"
+            return diff[s][:, i * C : (i + 1) * C].rearrange(view, u=2, e=2), p.rearrange(view, u=2, e=2)
 
-        def multiply_first(s):
-            d, p, g, c, t = factors(s)
-            nc.vector.tensor_tensor(out=te[g, c][:, t * C : (t + 1) * C], in0=d[:, 0], in1=p[:, 0], op=ALU.mult)
+        def multiply(s, i):
+            j, c, g, t = where(s)
+            d, p = factors(s, i)
+            if i == 1 and MOVED[g][c]:
+                nc.vector.tensor_tensor(out=e_block(s, 1, 0), in0=d[:, 0], in1=p[:, 0], op=ALU.mult)
+                nc.vector.tensor_tensor(out=e_block(s, 1, 1), in0=d[:, 1], in1=p[:, 1], op=ALU.mult)
+                return
+            nc.vector.tensor_tensor(out=tp[g, c][:, 0, t + i, :], in0=d, in1=p, op=ALU.mult)
 
-        def multiply_second(s):
-            d, p, g, c, t = factors(s)
-            blocks = tp[g, c][:].rearrange("p (b x) -> p b x", x=2 * P)
-            nc.vector.tensor_tensor(out=blocks[:, 2 * t + 2 : 2 * t + 10 : 7], in0=d[:, 1], in1=p[:, 1], op=ALU.mult)
-
-        def multiply_words(s):
-            d, p, g, c, t = factors(s)
-            e = te[g, c][:, t * C : (t + 2) * C].rearrange("p (i u x) -> p u i x", i=2, u=2)
-            nc.vector.tensor_tensor(out=e[:, 1, 0], in0=d[:, 0, 1], in1=p[:, 0, 1], op=ALU.mult)
-            nc.vector.tensor_tensor(out=e[:, 0], in0=d[:, :, 0], in1=p[:, :, 0], op=ALU.mult)
-
-        def multiply_part(s, part):
-            d, p, g, c, t = factors(s)
-            e = te[g, c][:, t * C : (t + 2) * C].rearrange("p (i u x) -> p u i x", i=2, u=2)
-            if part == 0:
-                nc.vector.tensor_tensor(out=e[:, 1, 0], in0=d[:, 0, 1], in1=p[:, 0, 1], op=ALU.mult)
-            else:
-                nc.vector.tensor_tensor(out=e[:, 0], in0=d[:, :, 0], in1=p[:, :, 0], op=ALU.mult)
-
-        def multiply_last(s, engine):
-            d, p, g, c, t = factors(s)
-            engine.tensor_tensor(out=e_block(g, c, t + 1, 1), in0=d[:, 1, 1], in1=p[:, 1, 1], op=ALU.mult)
-
-        def multiply_block(s, u):
-            d, p, g, c, t = factors(s)
-            nc.vector.tensor_tensor(out=e_block(g, c, t + 1, u), in0=d[:, 1, u], in1=p[:, 1, u], op=ALU.mult)
-
-        def multiply_shared(s):
-            d, p, g, c, t = factors(s)
-            multiply_first(s)
-            nc.vector.tensor_tensor(out=e_block(g, c, t + 1, 0), in0=d[:, 1, 0], in1=p[:, 1, 0], op=ALU.mult)
-            nc.gpsimd.tensor_tensor(out=e_block(g, c, t + 1, 1), in0=d[:, 1, 1], in1=p[:, 1, 1], op=ALU.mult)
+        def multiply_block(s, u, engine, i=1):
+            d, p = factors(s, i)
+            engine.tensor_tensor(out=e_block(s, i, u), in0=d[:, u], in1=p[:, u], op=ALU.mult)
 
         e_t = {}
         voc_mx = {}
 
         def e_turn(s, name="t0"):
-            j, i, g, t, c = where(2 * s)
             turned["e", s] = b = bank(name)
-            turn(b, [e_block(g, c, t + i, u).bitcast(F32) for i in range(2) for u in range(2)])
+            turn(b, [e_block(s, i, u).bitcast(F32) for i in range(2) for u in range(2)])
 
         def e_unturn(s):
-            e_t[s] = work.tile([P, 2 * C], BF16, name="e_t", align_bytes=64, bufs=2)
+            e_t[s] = work.tile([P, 2 * C], BF16, name="e_t", align_bytes=64, bufs=5)
             unturn(e_t[s][:], turned["e", s])
 
         def voc_quant(s):
-            voc_mx[s] = mx_tiles(work, "voc", 2 * P, 4)
-            quantise(voc_mx[s], e_t[s], 0, 2 * P)
+            voc_mx[ORDER[s]] = mx_tiles(work, "voc", 2 * P, 8)
+            quantise(voc_mx[ORDER[s]], e_t[s], 0, 2 * P)
 
-        def slot_turn(s, i):
-            j, i0, g, t, c = where(2 * s)
-            turned["slot", i] = b = bank("t0")
-            turn(b, [e_block(g, c, t + i, u).bitcast(F32) for u in range(2)])
+        held = {}
 
-        def slot_unturn(s, i):
-            if i == 0:
-                e_t[s] = work.tile([P, 2 * C], BF16, name="e_t", align_bytes=64, bufs=2)
-            nc.scalar.copy(
-                out=e_t[s][:, i * C : (i + 1) * C].bitcast(F32).rearrange("q (p u) -> q p u", u=2),
-                in_=turned["slot", i][:, : 2 * P].rearrange("q (u p) -> q p u", u=2),
-            )
-
-        def slot_quant(s, i):
-            if i == 0:
-                voc_mx[s] = mx_tiles(work, "voc", 2 * P, 4)
-            quantise(voc_mx[s], e_t[s], i * P, (i + 1) * P)
-
-        def dhid_pass(b, s, i, nh):
-            c = s % 4
+        def dhid_pass(j, x, c, name=None, a=0, b=C):
+            i, nh = divmod(x, 2)
+            if c == 0:
+                held[j, x, a] = bank(name or "d%d" % x)
+            n0 = nh * C
             nc.tensor.matmul_mx(
-                out=b[:],
-                lhsT=voc_mx[s][0][:, i * P : (i + 1) * P].bitcast(FP8X4),
-                lhsT_scale=voc_mx[s][1][:, i * P : (i + 1) * P],
-                rhs=u_codes[c][:, nh * 2 * C : (nh + 1) * 2 * C].bitcast(FP4X4),
-                rhs_scale=u_sc[:, c, nh * C : (nh + 1) * C],
+                out=held[j, x, a][:, : b - a],
+                lhsT=voc_mx[j, c][0][:, i * P : (i + 1) * P].bitcast(FP8X4),
+                lhsT_scale=voc_mx[j, c][1][:, i * P : (i + 1) * P],
+                rhs=u_codes[c][:, 2 * (n0 + a) : 2 * (n0 + b)].bitcast(FP4X4),
+                rhs_scale=u_sc[:, c, n0 + a : n0 + b],
                 start=c == 0,
                 stop=c == 3,
             )
 
-        def half_pass(b, s, half):
-            c = s % 4
-            a = C + half * 2 * P
-            nc.tensor.matmul_mx(
-                out=b[:, : 2 * P],
-                lhsT=voc_mx[s][0][:, P:].bitcast(FP8X4),
-                lhsT_scale=voc_mx[s][1][:, P:],
-                rhs=u_codes[c][:, 2 * a : 2 * (a + 2 * P)].bitcast(FP4X4),
-                rhs_scale=u_sc[:, c, a : a + 2 * P],
-                start=c == 0,
-                stop=c == 3,
-            )
-
-        def half_out(engine, b, half):
-            a = C + half * 2 * P
+        def copy_out(engine, src, dst, shape, width=C):
             if engine == "S":
-                r = work.tile([P, 2 * P], F32, name="res", bufs=6)
-                nc.scalar.copy(out=r[:], in_=b[:, : 2 * P])
-            else:
-                r = work.tile([P, 2 * P], F32, name="rows", bufs=4)
-                nc.vector.tensor_copy(out=r[:], in_=b[:, : 2 * P])
-            nc.sync.dma_start(out=slots(out_0, 3)[:, 1, a : a + 2 * P], in_=r[:])
-
-        def copy_out(engine, src, dst, shape):
-            if engine == "S":
-                r = work.tile([P, C], F32, name="res", bufs=6)
-            else:
-                r = work.tile([P, C], F32, name="rows", bufs=4)
-            if engine == "S":
+                r = work.tile([P, width], F32, name="res", bufs=5)
                 nc.scalar.copy(out=shape(r[:]), in_=src)
             else:
+                r = work.tile([P, width], F32, name="rows", bufs=4)
                 nc.vector.tensor_copy(out=shape(r[:]), in_=src)
             nc.sync.dma_start(out=dst, in_=r[:])
 
-        def dhid_out(engine, b, j, i, nh):
-            copy_out(engine, b[:], slots(out_0, j)[:, i, nh * C : (nh + 1) * C], lambda r: r)
-
-        groups = [(i, nh) for i in range(2) for nh in range(2)]
-        held = {}
-
-        def dhid_step(s, a=0, b=4):
-            for x in range(a, b):
-                i, nh = groups[x]
-                if s % 4 == 0:
-                    held[x] = bank("d%d" % x)
-                dhid_pass(held[x], s, i, nh)
-
-        def dhid_outs(j, engines):
-            for x, (i, nh) in enumerate(groups):
-                dhid_out(engines[x], held[x], j, i, nh)
+        def dhid_out(engine, j, x, a=0, b=C):
+            i, nh = divmod(x, 2)
+            copy_out(engine, held[j, x, a][:, : b - a], slots(out_0, j)[:, i, nh * C + a : nh * C + b], lambda r: r, b - a)
 
         tok_mx = {}
 
         def tok_weave(g, c, engine, a=0, b=C):
             key = ("tok", g, c)
+            if not MOVED[g][c]:
+                weave(key, tp[g, c][:, 0], engine, a, b)
+                return
             if a < 2 * P:
-                weave(key, te[g, c].rearrange("p (t v) -> p t v", t=4), engine, a, min(b, 2 * P))
+                weave(key, tp[g, c][:, 0], engine, a, min(b, 2 * P))
             if b > 2 * P:
                 a = max(a, 2 * P)
-                src = tp[g, c][:].rearrange("p (e h o v) -> p h e o v", e=2, h=2, o=2)[:, :, :, 0, a:b]
+                src = tp[g, c][:, :, 0:4:2, a:b].rearrange("p e h (c i) -> p c h e i", i=RUN)
                 o = woven[key][:, 4 * a : 4 * b].rearrange("p (c i h e) -> p c h e i", i=RUN, h=2, e=2)
-                src = src.rearrange("p h e (c i) -> p c h e i", i=RUN)
                 if engine == "V":
                     nc.vector.tensor_copy(out=o, in_=src)
                 else:
@@ -469,158 +350,239 @@ def tile_reverse_kl_backward_s8_kernel(
                 lambda x: x.rearrange("p (q u e) -> p q u e", u=2, e=2),
             )
 
+        nc.scalar.dma_start(
+            out=wsc[:].rearrange("p (g t) -> p g t", t=4), in_=w_scale.rearrange("(g p t) o -> p g (t o)", p=P, t=4)
+        )
+        nc.scalar.dma_start(out=cen[:].rearrange("p (g t) -> p g t", t=4), in_=centre.rearrange("(g p t) -> p g t", p=P, t=4))
+        nc.scalar.activation(out=cen32[:], in_=cen[:], func=ACT.Copy)
+        make_identity(nc, ident[:])
+        nc.scalar.copy(out=ident16[:], in_=ident[:])
+        nc.vector.memset(u_sc[:].rearrange("p g n -> p (g n)").bitcast(I32), 0)
+
+        load_w(0, 0, 1)
+        load_w(1, 0, 1)
+        load_hid(0)
+        load_w(0, 1, 1)
+        load_hid(1)
+        load_w(1, 1, 1)
+        load_tp(0, 0)
+        load_w(0, 2, 2)
+        load_tp(1, 0)
+        load_w(1, 2, 2)
+        load_tp(0, 1)
+        load_hid(2)
+        load_hid(3)
+        load_tp(1, 1)
+        load_u_scales()
+        load_u(0)
+        load_tp(0, 2)
+        load_u(1)
+        load_tp(1, 2)
+        load_u(2)
+        load_u(3)
+        load_act(0)
+        load_act(1)
+        load_tp(2, 0)
+        load_tp(3, 0)
+
         hid_turn(0, 0, "d0")
         hid_turn(0, 1, "d1")
-        widen(0, 0, "VVVS")
-        widen(1, 0, "VVSS")
-        w_weave(0, 0)
-        w_weave(1, 0)
-        widen(0, 1, "SSSS")
+        widen(0, "VVVS")
+        widen(1, "VVSS")
+        w_weave(0, "V", 0, C - P)
+        w_weave(0, "S", C - P, C)
+        w_weave(1, "V")
+        widen(2, "S---")
         hid_unturn(0, 0)
+        widen(2, "-S--")
         hid_unturn(0, 1)
-        w_quant(0, 0)
-        w_quant(1, 0)
-        widen(1, 1, "V---")
+        widen(2, "--S-")
+        w_quant(0)
+        w_quant(1)
+        widen(2, "---V")
         hid_quant(0)
-        z_mm(0)
-        z_mm(1)
-        probs_to_psum(0, "z2")
         hid_turn(1, 0, "d2")
         hid_turn(1, 1, "d3")
-        w_weave(0, 1)
-        for c in range(1, 4):
-            if c > 1:
-                widen(0, c, "SSSS")
-            if c == 3:
-                break
-            widen(1, c, "-SS-" if c == 1 else "SSS-")
-            widen(1, c, "---S", ON_GPSIMD[c], C)
+        z_mm(0)
+        z_mm(1)
+        probs_to_psum(0)
+        w_weave(2, "V")
 
-        def gate(c):
-            widen(1, c, "---V", 0, ON_GPSIMD[c])
-            w_weave(1, c, "G", 0, ON_GPSIMD[c])
-            w_quant(0, c)
+        def widen_ahead(k, planes):
+            widen(k, planes)
+            if planes[2] == "S":
+                widen(k, "---S", SHARE, C)
 
-        gate(1)
+        def gate(k):
+            widen(k, "---V", 0, SHARE)
+            w_weave(k, "G", 0, SHARE)
 
-        for s in range(3):
-            c = s + 1
+        def passes(j, c, xs=range(4)):
+            for x in xs:
+                dhid_pass(j, x, c)
+
+        def shared_multiply(s, engine):
+            multiply(s, 0)
+            multiply_block(s, 1, engine)
+            multiply_block(s, 0, nc.vector)
+
+        hid_unturn(1, 0)
+        hid_unturn(1, 1)
+        widen_ahead(3, "SSS-")
+        hid_quant(1)
+        gate(3)
+        w_quant(2)
+
+        quarters = [(tok_weave, (0, c), q) for c in range(2) for q in range(4)]
+        quarters = quarters + [(act_weave, (g,), q) for g in range(2) for q in range(4)]
+        quarters = quarters + [(tok_weave, (0, c), q) for c in (2, 3) for q in range(4)]
+        filled = []
+
+        def fill(n):
+            for f, key, q in quarters[len(filled) : len(filled) + n]:
+                f(*key, "S", q * P, (q + 1) * P)
+                filled.append(q)
+
+        for s in range(5):
+            k = s + 3
             subtract(2 * s)
+            z_mm(2 * s + 2)
             subtract(2 * s + 1)
-            z_mm(2 * c, (0,))
-            z_mm(2 * c + 1, (0,))
-            if c < 3:
-                multiply_first(s)
-                multiply_second(s)
-                w_weave(1, c, "V", ON_GPSIMD[c], C)
-                if s == 0:
-                    w_weave(0, 2)
-                else:
-                    w_weave(0, 3, "V", 0, C // 2)
-                w_quant(1, c)
-                if s == 1:
-                    hid_turn(3, 0, "z2")
-                e_turn(s)
-                if s == 0:
-                    probs_to_psum(1, "z2")
-                z_mm(2 * c, (1,))
-                z_mm(2 * c + 1, (1,))
+            z_mm(2 * s + 3)
+            if REST[s] == "S":
+                w_weave(k, "S", SHARE, C)
+            if s < 4:
+                widen_ahead(k + 1, "S---" if REST[s] == "S" else "SS--")
             else:
-                w_quant(1, c)
-                multiply_shared(s)
-                z_mm(2 * c, (1,))
-                z_mm(2 * c + 1, (1,))
-            if s == 0:
-                e_unturn(0)
-                widen(1, 3, "SSS-")
-                widen(1, 3, "---S", ON_GPSIMD[3], C)
-                hid_turn(2, 0, "d0")
-                hid_turn(2, 1, "d1")
-                hid_turn(3, 1, "t0")
-                gate(2)
-                hid_unturn(3, 1)
-                hid_unturn(1, 0)
-                hid_unturn(1, 1)
-            if s == 1:
-                e_unturn(1)
-                hid_unturn(2, 0)
-                hid_unturn(2, 1)
-                voc_quant(0)
-                w_weave(0, 3, "V", C // 2, C)
-                hid_quant(1)
-                voc_quant(1)
-                for x in (2, 0):
-                    dhid_step(0, x, x + 2)
-                    dhid_step(1, x, x + 2)
-                gate(3)
-                w_weave(1, 3, "S", ON_GPSIMD[3], C)
-                hid_unturn(3, 0)
-        act_weave(0, "S")
-        act_weave(1, "S", 0, R // 2)
-        z_mm(8)
-
-        def extras(s):
-            if s == 6:
-                hid_quant(2)
-            if s == 7:
-                act_quant(0)
-            if s == 8:
-                act_quant(1)
-            if s == 9:
-                tok_quant(0, 0)
-            if s == 10:
-                hid_quant(3)
-            if s == 11:
-                tok_quant(0, 1)
-
-        for s in range(3, 12):
-            j, c = divmod(s, 4)
-            subtract(2 * s)
-            subtract(2 * s + 1)
-            extras(s)
-            z_mm(2 * s + Z_BANKS)
-            if s == 3:
-                e_turn(2)
-                e_unturn(2)
-            z_mm(2 * s + 1 + Z_BANKS)
-            if s > 3:
-                e_turn(s - 1)
+                fill(1)
+            if s > 0:
                 e_unturn(s - 1)
             if s < 4:
-                multiply_shared(s)
-            else:
-                multiply_words(s)
-                multiply_last(s, nc.gpsimd)
-                voc_quant(s - 2)
-                dhid_step(s - 2)
-                if s % 4 == 1:
-                    dhid_outs(s // 4 - 1, "SSSS")
-                if s == 5:
-                    for late_c in range(3, 4):
-                        load_tp4(late_c)
+                widen_ahead(k + 1, "-SS-" if REST[s] == "S" else "--S-")
+            if s in (2, 3):
+                hid_unturn(s, 0)
+                hid_unturn(s, 1)
             if s == 3:
-                act_weave(1, "S", R // 2, R)
-            if s in (4, 6, 7):
-                tok_weave(0, max(s - 5, 0), "S")
-            if s in (8, 10):
-                tok_weave(0, 3, "S", (s - 8) * P, (s - 6) * P)
+                passes(0, 0, (0, 1))
+            if s == 4:
+                passes(0, 0, (2, 3))
+                passes(0, 1, (2, 3))
+            multiply(s, 0)
+            multiply(s, 1)
+            if s < 4:
+                probs_to_psum(s + 1)
+            e_turn(s)
+            if s in (1, 2):
+                hid_turn(s + 1, 0, "d%d" % (2 * s - 2))
+                hid_turn(s + 1, 1, "d%d" % (2 * s - 1))
+            if REST[s] == "V":
+                w_weave(k, "V", SHARE, C)
+            if s in (1, 3):
+                voc_quant(s - 1)
+            if s == 3:
+                passes(0, 1, (0, 1))
+            if s < 4:
+                gate(k + 1)
+            w_quant(k)
 
-        late = {}
+        fill(3)
+        e_unturn(4)
+        fill(4)
 
-        def late_passes(names, steps):
-            for s in steps:
-                for x in names:
-                    if x not in late:
-                        late[x] = bank(("z2", "z0", "z1", "d0")[x])
-                    dhid_pass(late[x], s, *groups[x])
+        subtract(10)
+        z_mm(12)
+        subtract(11)
+        z_mm(13)
+        hid_quant(2)
+        voc_quant(4)
+        passes(0, 2)
+        shared_multiply(5, nc.gpsimd)
 
-        def dups(c, rows, names=("d0", "d1", "d2", "d3")):
-            for r in rows:
-                dup(names[r], r, c)
+        subtract(12)
+        z_mm(14)
+        subtract(13)
+        z_mm(15)
+        multiply(6, 0)
+        multiply(6, 1)
+        e_turn(6)
+        e_turn(5, "z2")
+        fill(3)
+        e_unturn(6)
+        e_unturn(5)
+        fill(2)
 
-        def dup_outs(c, rows):
-            for r in rows:
-                dup_out("S", r, c)
+        subtract(14)
+        z_mm(16)
+        subtract(15)
+        z_mm(17)
+        voc_quant(1)
+        voc_quant(6)
+        passes(0, 3)
+        shared_multiply(7, nc.gpsimd)
+        for x in range(4):
+            dhid_out("S", 0, x)
+
+        subtract(16)
+        z_mm(18)
+        subtract(17)
+        z_mm(19)
+        voc_quant(3)
+        voc_quant(5)
+        e_turn(7)
+        e_unturn(7)
+        z_mm(20)
+        for x in range(2):
+            for c in range(3):
+                dhid_pass(1, x, c)
+        hid_quant(3)
+        tok_quant(0, 0)
+        shared_multiply(8, nc.gpsimd)
+        fill(4)
+
+        subtract(18)
+        subtract(19)
+        voc_quant(7)
+        z_mm(21)
+        passes(1, 3, range(2))
+        z_mm(22)
+        e_turn(8)
+        dhid_out("S", 1, 0)
+        dhid_out("S", 1, 1)
+        fill(1)
+        e_unturn(8)
+        for x in range(2, 4):
+            for c in range(4):
+                dhid_pass(1, x, c)
+        tok_quant(0, 1)
+        act_quant(0)
+        shared_multiply(9, nc.gpsimd)
+        fill(2)
+        dhid_out("S", 1, 2)
+        dhid_out("S", 1, 3)
+
+        subtract(20)
+        subtract(21)
+        z_mm(23)
+        z_mm(24)
+        e_turn(9)
+        fill(1)
+        e_unturn(9)
+        voc_quant(8)
+        passes(2, 0)
+        act_quant(1)
+        tok_quant(0, 2)
+        shared_multiply(10, nc.gpsimd)
+        fill(3)
+
+        subtract(22)
+        subtract(23)
+        z_mm(25)
+        z_mm(26)
+        e_turn(10)
+        e_unturn(10)
+        voc_quant(9)
+        passes(2, 1)
+        shared_multiply(11, nc.gpsimd)
 
         subtract(24)
         subtract(25)
@@ -629,77 +591,88 @@ def tile_reverse_kl_backward_s8_kernel(
         z_mm(27)
         z_mm(28)
         voc_quant(10)
-        dhid_step(10)
-        multiply_part(12, 0)
-        tok_quant(0, 2)
-        multiply_part(12, 1)
-        multiply_last(12, nc.gpsimd)
+        passes(2, 2)
+        multiply_block(12, 0, nc.vector)
+        tok_quant(0, 3)
+        multiply(12, 0)
+        multiply_block(12, 1, nc.gpsimd)
         voc_quant(11)
-        dhid_step(11)
-        tok_weave(1, 0, "S", 0, 2 * P)
+        passes(2, 3)
+        tok_weave(1, 0, "S", 0, C // 2)
 
         subtract(26)
         subtract(27)
-        tok_weave(1, 0, "V", 2 * P, C)
-        multiply_part(13, 0)
+        tok_weave(1, 0, "V", C // 2, C)
+        multiply_block(13, 0, nc.vector)
         tok_quant(1, 0)
         z_mm(29)
         z_mm(30)
-        dhid_outs(2, "SSSS")
-        dups(0, range(4))
-        multiply_part(13, 1)
-        multiply_last(13, nc.gpsimd)
-        tok_quant(0, 3)
-        tok_weave(1, 1, "S", 0, 2 * P)
-        dup_outs(0, range(4))
+        for x in range(4):
+            dhid_out("S", 2, x)
+        for r in range(4):
+            dup("d%d" % r, r, 0)
+        multiply(13, 0)
+        multiply_block(13, 1, nc.gpsimd)
+        tok_weave(1, 1, "S", 0, C // 2)
+        for r in range(4):
+            dup_out("S", r, 0)
 
         subtract(28)
         subtract(29)
-        tok_weave(1, 1, "V", 2 * P, C)
-        multiply_words(14)
+        tok_weave(1, 1, "V", C // 2, C)
+        multiply_block(14, 0, nc.vector)
+        multiply(14, 0)
         tok_quant(1, 1)
         z_mm(31)
         e_turn(12, "z2")
         e_turn(13)
         e_unturn(12)
         e_unturn(13)
-        dups(1, range(4))
-        dup_outs(1, range(4))
-        multiply_last(14, nc.vector)
+        for r in range(4):
+            dup("d%d" % r, r, 1)
+            dup_out("S", r, 1)
+        multiply_block(14, 1, nc.vector)
         e_turn(14)
         e_unturn(14)
         tok_weave(1, 2, "V")
         voc_quant(12)
         tok_quant(1, 2)
         voc_quant(13)
-        late_passes((0,), (12, 13))
+        dhid_pass(3, 0, 0, "z2")
+        dhid_pass(3, 0, 1)
 
         subtract(30)
         subtract(31)
-        dups(2, range(3))
-        dup_outs(2, range(2))
-        multiply_words(15)
+        for r in range(3):
+            dup("d%d" % r, r, 2)
+        dup_out("S", 0, 2)
+        dup_out("S", 1, 2)
+        multiply(15, 0)
+        multiply_block(15, 0, nc.vector)
         voc_quant(14)
-        multiply_last(15, nc.vector)
+        multiply_block(15, 1, nc.vector)
         e_turn(15)
         e_unturn(15)
-        dups(2, range(3, 4))
-        dup_outs(2, range(2, 4))
-        late_passes((0,), (14,))
-        late_passes((1,), (12, 13, 14))
+        dup("d3", 3, 2)
+        dup_out("S", 2, 2)
+        dup_out("S", 3, 2)
+        dhid_pass(3, 0, 2)
+        for c in range(3):
+            dhid_pass(3, 1, c, "z0")
         tok_weave(1, 3, "V")
         voc_quant(15)
         tok_quant(1, 3)
-        late_passes((0, 1), (15,))
-        dhid_out("S", late[0], 3, *groups[0])
-        dhid_out("V", late[1], 3, *groups[1])
+        dhid_pass(3, 0, 3)
+        dhid_pass(3, 1, 3)
+        dhid_out("S", 3, 0)
+        dhid_out("V", 3, 1)
         for r in range(4):
             dup(("d1", "d2", "d3", "t0")[r], r, 3)
             dup_out("SV"[r % 2], r, 3)
-        late_passes((2,), range(12, 16))
-        dhid_out("S", late[2], 3, *groups[2])
-        for half, name, engine in ((0, "d0", "V"), (1, "z2", "S")):
-            b = bank(name)
-            for s in range(12, 16):
-                half_pass(b, s, half)
-            half_out(engine, b, half)
+        for c in range(4):
+            dhid_pass(3, 2, c, "z1")
+        dhid_out("S", 3, 2)
+        for a, name, engine in ((0, "d0", "V"), (C // 2, "z2", "S")):
+            for c in range(4):
+                dhid_pass(3, 3, c, name, a, a + C // 2)
+            dhid_out(engine, 3, 3, a, a + C // 2)

@@ -20,7 +20,6 @@ C = 512
 FLOPS = 2 * M * D * V * 2 + 2 * M * R * V
 RUN = 8
 SHARE = 336
-REST = "SSVVS"
 Z3_FROM = 18
 MOVED = ((False, False, True, True), (True,) * 4)
 BLOCKS = [(0, 0, 1), (0, 1, 1), (0, 2, 2), (1, 0, 4)]
@@ -59,9 +58,11 @@ def tile_reverse_kl_backward_s8_kernel(
         w_view = w_bytes.rearrange("(g p t) v -> g p t v", p=P, t=4)
         w_raw = {}
 
-        def load_w(kg, c, n):
+        def load_w(kg, c, n, pieces=1):
             wb = keep.tile([P, 4, n * C], U8, name="w_bytes_%d_%d" % (kg, c))
-            nc.sync.dma_start(out=wb[:], in_=w_view[kg][:, :, c * C : (c + n) * C])
+            for a in range(0, 4, 4 // pieces):
+                planes = slice(a, a + 4 // pieces)
+                nc.sync.dma_start(out=wb[:, planes], in_=w_view[kg][:, planes, c * C : (c + n) * C])
             for i in range(n):
                 w_raw[kg, c + i] = wb[:, :, i * C : (i + 1) * C]
 
@@ -310,6 +311,8 @@ def tile_reverse_kl_backward_s8_kernel(
                 weave(key, tp[g, c][:, 0], engine, a, min(b, 2 * P))
             if b > 2 * P:
                 a = max(a, 2 * P)
+                if key not in woven:
+                    woven[key] = work.tile([P, 4 * C], BF16, name="woven", align_bytes=64, bufs=5)
                 src = tp[g, c][:, :, 0:4:2, a:b].rearrange("p e h (c i) -> p c h e i", i=RUN)
                 o = woven[key][:, 4 * a : 4 * b].rearrange("p (c i h e) -> p c h e i", i=RUN, h=2, e=2)
                 if engine == "V":
@@ -408,13 +411,8 @@ def tile_reverse_kl_backward_s8_kernel(
         probs_to_psum(0)
         w_weave(2, "V")
 
-        def widen_ahead(k, planes):
-            widen(k, planes)
-            if planes[2] == "S":
-                widen(k, "---S", SHARE, C)
-
         def gate(k):
-            widen(k, "---V", 0, SHARE)
+            widen(k, "---V")
             w_weave(k, "G", 0, SHARE)
 
         def passes(j, c, xs=range(4)):
@@ -428,14 +426,14 @@ def tile_reverse_kl_backward_s8_kernel(
 
         hid_unturn(1, 0)
         hid_unturn(1, 1)
-        widen_ahead(3, "SSS-")
+        widen(3, "SSS-")
         hid_quant(1)
         gate(3)
         w_quant(2)
 
         quarters = [(tok_weave, (0, c), q) for c in range(2) for q in range(4)]
         quarters = quarters + [(act_weave, (g,), q) for g in range(2) for q in range(4)]
-        quarters = quarters + [(tok_weave, (0, c), q) for c in (2, 3) for q in range(4)]
+        quarters = quarters + [(tok_weave, (0, c), q) for c in (2, 3) for q in range(6 - c)]
         filled = []
 
         def fill(n):
@@ -449,24 +447,25 @@ def tile_reverse_kl_backward_s8_kernel(
             z_mm(2 * s + 2)
             subtract(2 * s + 1)
             z_mm(2 * s + 3)
-            if REST[s] == "S":
-                w_weave(k, "S", SHARE, C)
             if s < 4:
-                widen_ahead(k + 1, "S---" if REST[s] == "S" else "SS--")
+                widen(k + 1, "S---")
             else:
-                fill(1)
+                hid_unturn(3, 0)
+            w_weave(k, "S", SHARE, C)
             if s > 0:
                 e_unturn(s - 1)
             if s < 4:
-                widen_ahead(k + 1, "-SS-" if REST[s] == "S" else "--S-")
+                widen(k + 1, "-SS-")
+            else:
+                hid_unturn(3, 1)
             if s in (2, 3):
-                hid_unturn(s, 0)
-                hid_unturn(s, 1)
+                hid_unturn(2, s - 2)
             if s == 3:
-                passes(0, 0, (0, 1))
+                passes(0, 0, (0,))
             if s == 4:
-                passes(0, 0, (2, 3))
-                passes(0, 1, (2, 3))
+                passes(0, 0, (1,))
+                passes(0, 1, (1,))
+                passes(0, 0, (2,))
             multiply(s, 0)
             multiply(s, 1)
             if s < 4:
@@ -475,24 +474,25 @@ def tile_reverse_kl_backward_s8_kernel(
             if s in (1, 2):
                 hid_turn(s + 1, 0, "d%d" % (2 * s - 2))
                 hid_turn(s + 1, 1, "d%d" % (2 * s - 1))
-            if REST[s] == "V":
-                w_weave(k, "V", SHARE, C)
             if s in (1, 3):
                 voc_quant(s - 1)
             if s == 3:
-                passes(0, 1, (0, 1))
+                passes(0, 1, (0,))
             if s < 4:
                 gate(k + 1)
             w_quant(k)
 
-        fill(3)
+        passes(0, 1, (2,))
+        passes(0, 0, (3,))
+        fill(2)
         e_unturn(4)
-        fill(4)
+        fill(5)
 
         subtract(10)
         z_mm(12)
         subtract(11)
         z_mm(13)
+        passes(0, 1, (3,))
         hid_quant(2)
         voc_quant(4)
         passes(0, 2)
@@ -506,7 +506,7 @@ def tile_reverse_kl_backward_s8_kernel(
         multiply(6, 1)
         e_turn(6)
         e_turn(5, "z2")
-        fill(3)
+        fill(2)
         e_unturn(6)
         e_unturn(5)
         fill(2)
@@ -516,6 +516,7 @@ def tile_reverse_kl_backward_s8_kernel(
         subtract(15)
         z_mm(17)
         voc_quant(1)
+        voc_quant(3)
         voc_quant(6)
         passes(0, 3)
         shared_multiply(7, nc.gpsimd)
@@ -526,7 +527,6 @@ def tile_reverse_kl_backward_s8_kernel(
         z_mm(18)
         subtract(17)
         z_mm(19)
-        voc_quant(3)
         voc_quant(5)
         e_turn(7)
         e_unturn(7)
@@ -569,8 +569,8 @@ def tile_reverse_kl_backward_s8_kernel(
         e_unturn(9)
         voc_quant(8)
         passes(2, 0)
+        tok_weave(0, 3, "V", 3 * P, C)
         act_quant(1)
-        tok_quant(0, 2)
         shared_multiply(10, nc.gpsimd)
         fill(3)
 
@@ -580,8 +580,10 @@ def tile_reverse_kl_backward_s8_kernel(
         z_mm(26)
         e_turn(10)
         e_unturn(10)
+        fill(1)
         voc_quant(9)
         passes(2, 1)
+        tok_quant(0, 2)
         shared_multiply(11, nc.gpsimd)
 
         subtract(24)
@@ -647,6 +649,7 @@ def tile_reverse_kl_backward_s8_kernel(
             dup("d%d" % r, r, 2)
         dup_out("S", 0, 2)
         dup_out("S", 1, 2)
+        dup_out("S", 2, 2)
         multiply(15, 0)
         multiply_block(15, 0, nc.vector)
         voc_quant(14)
@@ -654,7 +657,6 @@ def tile_reverse_kl_backward_s8_kernel(
         e_turn(15)
         e_unturn(15)
         dup("d3", 3, 2)
-        dup_out("S", 2, 2)
         dup_out("S", 3, 2)
         dhid_pass(3, 0, 2)
         for c in range(3):

@@ -20,7 +20,7 @@ C = 512
 FLOPS = 2 * M * D * V * 2 + 2 * M * R * V
 RUN = 8
 SHARE = 336
-Z3_FROM = 18
+Z3_FROM = 12
 MOVED = ((False, False, True, True), (True,) * 4)
 BLOCKS = [(0, 0, 1), (0, 1, 1), (0, 2, 2), (1, 0, 4)]
 ORDER = [(j, c) for c in range(4) for j in (0, 1)] + [(j, c) for j in (2, 3) for c in range(4)]
@@ -152,8 +152,8 @@ def tile_reverse_kl_backward_s8_kernel(
         def w_weave(k, engine, a=0, b=C):
             weave(("w", k), wide[k][:], engine, a, b)
 
-        def w_quant(k):
-            quantise(w_mx[k], woven["w", k], 0, C)
+        def w_quant(k, a=0, b=C):
+            quantise(w_mx[k], woven["w", k], a, b)
 
         def turn(b, words):
             for i, w in enumerate(words):
@@ -187,21 +187,21 @@ def tile_reverse_kl_backward_s8_kernel(
 
         zb = {}
 
-        def z_mm(n, halves=(0, 1)):
+        def z_mm(n, parts=((0, 0, C), (1, 0, C))):
             s, i = divmod(n, 2)
             j, c, g, t = where(s)
             if n not in zb:
                 zb[n] = bank("z%d" % (n % 2 if n < Z3_FROM else n % 3))
-            for kg in halves:
+            for kg, a, b in parts:
                 cols = slice((2 * kg + i) * P, (2 * kg + i + 1) * P)
                 nc.tensor.matmul_mx(
-                    out=zb[n][:],
+                    out=zb[n][:, a:b],
                     lhsT=hid_mx[j][0][:, cols].bitcast(FP8X4),
                     lhsT_scale=hid_mx[j][1][:, cols],
-                    rhs=w_mx[2 * c + kg][0][:].bitcast(FP8X4),
-                    rhs_scale=w_mx[2 * c + kg][1][:],
+                    rhs=w_mx[2 * c + kg][0][:, a:b].bitcast(FP8X4),
+                    rhs_scale=w_mx[2 * c + kg][1][:, a:b],
                     start=kg == 0,
-                    stop=kg == 1,
+                    stop=kg == 1 and a == 0,
                 )
 
         diff = {}
@@ -267,7 +267,7 @@ def tile_reverse_kl_backward_s8_kernel(
             unturn(e_t[s][:], turned["e", s])
 
         def voc_quant(s):
-            voc_mx[ORDER[s]] = mx_tiles(work, "voc", 2 * P, 8)
+            voc_mx[ORDER[s]] = mx_tiles(work, "voc", 2 * P, 6)
             quantise(voc_mx[ORDER[s]], e_t[s], 0, 2 * P)
 
         held = {}
@@ -289,7 +289,7 @@ def tile_reverse_kl_backward_s8_kernel(
 
         def copy_out(engine, src, dst, shape, width=C):
             if engine == "S":
-                r = work.tile([P, width], F32, name="res", bufs=5)
+                r = work.tile([P, width], F32, name="res", bufs=6)
                 nc.scalar.copy(out=shape(r[:]), in_=src)
             else:
                 r = work.tile([P, width], F32, name="rows", bufs=4)
@@ -372,8 +372,8 @@ def tile_reverse_kl_backward_s8_kernel(
         load_w(0, 2, 2)
         load_tp(1, 0)
         load_w(1, 2, 2)
-        load_tp(0, 1)
         load_hid(2)
+        load_tp(0, 1)
         load_hid(3)
         load_tp(1, 1)
         load_u_scales()
@@ -403,13 +403,14 @@ def tile_reverse_kl_backward_s8_kernel(
         w_quant(0)
         w_quant(1)
         widen(2, "---V")
+        widen(3, "V---")
         hid_quant(0)
         hid_turn(1, 0, "d2")
         hid_turn(1, 1, "d3")
         z_mm(0)
         z_mm(1)
         probs_to_psum(0)
-        w_weave(2, "V")
+        w_weave(2, "V", 0, C - 96)
 
         def gate(k):
             widen(k, "---V")
@@ -426,14 +427,15 @@ def tile_reverse_kl_backward_s8_kernel(
 
         hid_unturn(1, 0)
         hid_unturn(1, 1)
-        widen(3, "SSS-")
+        w_weave(2, "S", C - 96, C)
+        widen(3, "-SS-")
         hid_quant(1)
         gate(3)
         w_quant(2)
 
         quarters = [(tok_weave, (0, c), q) for c in range(2) for q in range(4)]
         quarters = quarters + [(act_weave, (g,), q) for g in range(2) for q in range(4)]
-        quarters = quarters + [(tok_weave, (0, c), q) for c in (2, 3) for q in range(6 - c)]
+        quarters = quarters + [(tok_weave, (0, c), q) for c in (2, 3) for q in range(2 * c - 2)]
         filled = []
 
         def fill(n):
@@ -458,8 +460,8 @@ def tile_reverse_kl_backward_s8_kernel(
                 widen(k + 1, "-SS-")
             else:
                 hid_unturn(3, 1)
-            if s in (2, 3):
-                hid_unturn(2, s - 2)
+            if s in (1, 3):
+                hid_unturn(2, s // 2)
             if s == 3:
                 passes(0, 0, (0,))
             if s == 4:
@@ -471,9 +473,10 @@ def tile_reverse_kl_backward_s8_kernel(
             if s < 4:
                 probs_to_psum(s + 1)
             e_turn(s)
-            if s in (1, 2):
-                hid_turn(s + 1, 0, "d%d" % (2 * s - 2))
-                hid_turn(s + 1, 1, "d%d" % (2 * s - 1))
+            if s < 3:
+                hid_turn(2 + s // 2, s % 2, "d%d" % s)
+            if s == 1:
+                hid_turn(3, 1, "d3")
             if s in (1, 3):
                 voc_quant(s - 1)
             if s == 3:
@@ -498,35 +501,35 @@ def tile_reverse_kl_backward_s8_kernel(
         passes(0, 2)
         shared_multiply(5, nc.gpsimd)
 
-        subtract(12)
         z_mm(14)
-        subtract(13)
+        subtract(12)
         z_mm(15)
+        subtract(13)
         multiply(6, 0)
         multiply(6, 1)
         e_turn(6)
-        e_turn(5, "z2")
+        z_mm(16)
         fill(2)
         e_unturn(6)
-        e_unturn(5)
         fill(2)
 
         subtract(14)
-        z_mm(16)
-        subtract(15)
         z_mm(17)
+        subtract(15)
+        e_turn(5)
+        e_unturn(5)
         voc_quant(1)
         voc_quant(3)
         voc_quant(6)
         passes(0, 3)
+        z_mm(18)
         shared_multiply(7, nc.gpsimd)
         for x in range(4):
             dhid_out("S", 0, x)
 
         subtract(16)
-        z_mm(18)
-        subtract(17)
         z_mm(19)
+        subtract(17)
         voc_quant(5)
         e_turn(7)
         e_unturn(7)
@@ -548,7 +551,6 @@ def tile_reverse_kl_backward_s8_kernel(
         e_turn(8)
         dhid_out("S", 1, 0)
         dhid_out("S", 1, 1)
-        fill(1)
         e_unturn(8)
         for x in range(2, 4):
             for c in range(4):
@@ -556,7 +558,7 @@ def tile_reverse_kl_backward_s8_kernel(
         tok_quant(0, 1)
         act_quant(0)
         shared_multiply(9, nc.gpsimd)
-        fill(2)
+        fill(3)
         dhid_out("S", 1, 2)
         dhid_out("S", 1, 3)
 
@@ -565,11 +567,10 @@ def tile_reverse_kl_backward_s8_kernel(
         z_mm(23)
         z_mm(24)
         e_turn(9)
-        fill(1)
         e_unturn(9)
+        tok_weave(0, 2, "V", C // 2, C)
         voc_quant(8)
         passes(2, 0)
-        tok_weave(0, 3, "V", 3 * P, C)
         act_quant(1)
         shared_multiply(10, nc.gpsimd)
         fill(3)
@@ -581,9 +582,9 @@ def tile_reverse_kl_backward_s8_kernel(
         e_turn(10)
         e_unturn(10)
         fill(1)
+        tok_quant(0, 2)
         voc_quant(9)
         passes(2, 1)
-        tok_quant(0, 2)
         shared_multiply(11, nc.gpsimd)
 
         subtract(24)

@@ -19,7 +19,7 @@ P = 128
 C = 512
 FLOPS = 2 * M * D * V * 2 + 2 * M * R * V
 RUN = 8
-SHARE = 336
+SHARE = (336, 336, 336, 336, 336)
 Z3_FROM = 12
 MOVED = ((False, False, True, True), (True,) * 4)
 BLOCKS = [(0, 0, 1), (0, 1, 1), (0, 2, 2), (1, 0, 4)]
@@ -92,7 +92,7 @@ def tile_reverse_kl_backward_s8_kernel(
         def load_tp(j, c):
             g, h = divmod(j, 2)
             tile, n = tp["block", g, c]
-            for x, src in enumerate((teach, probs)):
+            for x, src in ((1, probs), (0, teach)) if g == 0 else ((0, teach), (1, probs)):
                 a = (4 * x + 2 * h) * n * C
                 nc.sync.dma_start(
                     out=tile[:, a : a + 2 * n * C].rearrange("p (t v) -> p t v", t=2),
@@ -414,7 +414,7 @@ def tile_reverse_kl_backward_s8_kernel(
 
         def gate(k):
             widen(k, "---V")
-            w_weave(k, "G", 0, SHARE)
+            w_weave(k, "G", 0, SHARE[k - 3])
 
         def passes(j, c, xs=range(4)):
             for x in xs:
@@ -453,7 +453,7 @@ def tile_reverse_kl_backward_s8_kernel(
                 widen(k + 1, "S---")
             else:
                 hid_unturn(3, 0)
-            w_weave(k, "S", SHARE, C)
+            w_weave(k, "S", SHARE[s], C)
             if s > 0:
                 e_unturn(s - 1)
             if s < 4:
@@ -622,9 +622,10 @@ def tile_reverse_kl_backward_s8_kernel(
 
         subtract(28)
         subtract(29)
+        multiply_block(14, 1, nc.vector, 0)
         tok_weave(1, 1, "V", C // 2, C)
         multiply_block(14, 0, nc.vector)
-        multiply(14, 0)
+        multiply_block(14, 0, nc.vector, 0)
         tok_quant(1, 1)
         z_mm(31)
         e_turn(12, "z2")

@@ -435,7 +435,7 @@ def tile_reverse_kl_backward_s8_kernel(
 
         quarters = [(tok_weave, (0, c), q) for c in range(2) for q in range(4)]
         quarters = quarters + [(act_weave, (g,), q) for g in range(2) for q in range(4)]
-        quarters = quarters + [(tok_weave, (0, c), q) for c in (2, 3) for q in range(2 * c - 2)]
+        quarters = quarters + [(tok_weave, (0, c), q) for c in (2, 3) for q in range(4)]
         filled = []
 
         def fill(n):
@@ -540,14 +540,14 @@ def tile_reverse_kl_backward_s8_kernel(
         hid_quant(3)
         tok_quant(0, 0)
         shared_multiply(8, nc.gpsimd)
-        fill(4)
+        fill(5)
 
         subtract(18)
         subtract(19)
         voc_quant(7)
         z_mm(21)
-        passes(1, 3, range(2))
         z_mm(22)
+        passes(1, 3, range(2))
         e_turn(8)
         dhid_out("S", 1, 0)
         dhid_out("S", 1, 1)
@@ -558,9 +558,10 @@ def tile_reverse_kl_backward_s8_kernel(
         tok_quant(0, 1)
         act_quant(0)
         shared_multiply(9, nc.gpsimd)
-        fill(3)
+        fill(2)
         dhid_out("S", 1, 2)
         dhid_out("S", 1, 3)
+        fill(1)
 
         subtract(20)
         subtract(21)
@@ -568,10 +569,9 @@ def tile_reverse_kl_backward_s8_kernel(
         z_mm(24)
         e_turn(9)
         e_unturn(9)
-        tok_weave(0, 2, "V", C // 2, C)
+        act_quant(1)
         voc_quant(8)
         passes(2, 0)
-        act_quant(1)
         shared_multiply(10, nc.gpsimd)
         fill(3)
 
@@ -580,12 +580,16 @@ def tile_reverse_kl_backward_s8_kernel(
         z_mm(25)
         z_mm(26)
         e_turn(10)
+        fill(1)
         e_unturn(10)
         fill(1)
-        tok_quant(0, 2)
+        multiply_block(11, 1, nc.vector, 0)
+        multiply_block(11, 0, nc.vector)
         voc_quant(9)
         passes(2, 1)
-        shared_multiply(11, nc.gpsimd)
+        multiply_block(11, 0, nc.vector, 0)
+        multiply_block(11, 1, nc.gpsimd)
+        tok_quant(0, 2)
 
         subtract(24)
         subtract(25)
@@ -593,11 +597,12 @@ def tile_reverse_kl_backward_s8_kernel(
         e_unturn(11)
         z_mm(27)
         z_mm(28)
+        multiply_block(12, 1, nc.vector, 0)
         voc_quant(10)
         passes(2, 2)
         multiply_block(12, 0, nc.vector)
         tok_quant(0, 3)
-        multiply(12, 0)
+        multiply_block(12, 0, nc.vector, 0)
         multiply_block(12, 1, nc.gpsimd)
         voc_quant(11)
         passes(2, 3)
@@ -651,7 +656,6 @@ def tile_reverse_kl_backward_s8_kernel(
             dup("d%d" % r, r, 2)
         dup_out("S", 0, 2)
         dup_out("S", 1, 2)
-        dup_out("S", 2, 2)
         multiply(15, 0)
         multiply_block(15, 0, nc.vector)
         voc_quant(14)
@@ -659,6 +663,7 @@ def tile_reverse_kl_backward_s8_kernel(
         e_turn(15)
         e_unturn(15)
         dup("d3", 3, 2)
+        dup_out("S", 2, 2)
         dup_out("S", 3, 2)
         dhid_pass(3, 0, 2)
         for c in range(3):

@@ -19,7 +19,7 @@ P = 128
 C = 512
 FLOPS = 2 * M * D * V * 2 + 2 * M * R * V
 RUN = 8
-SHARE = (336, 336, 336, 336, 336)
+SHARE = (336, 352, 352, 352, 336)
 Z3_FROM = 12
 MOVED = ((False, False, True, True), (True,) * 4)
 BLOCKS = [(0, 0, 1), (0, 1, 1), (0, 2, 2), (1, 0, 4)]
@@ -412,8 +412,10 @@ def tile_reverse_kl_backward_s8_kernel(
         probs_to_psum(0)
         w_weave(2, "V", 0, C - 96)
 
+        PIECE = 384
+
         def gate(k):
-            widen(k, "---V")
+            widen(k, "---V", 0, PIECE)
             w_weave(k, "G", 0, SHARE[k - 3])
 
         def passes(j, c, xs=range(4)):
@@ -428,6 +430,7 @@ def tile_reverse_kl_backward_s8_kernel(
         hid_unturn(1, 0)
         hid_unturn(1, 1)
         w_weave(2, "S", C - 96, C)
+        widen(3, "---S", PIECE, C)
         widen(3, "-SS-")
         hid_quant(1)
         gate(3)
@@ -457,6 +460,7 @@ def tile_reverse_kl_backward_s8_kernel(
             if s > 0:
                 e_unturn(s - 1)
             if s < 4:
+                widen(k + 1, "---S", PIECE, C)
                 widen(k + 1, "-SS-")
             else:
                 hid_unturn(3, 1)
@@ -473,10 +477,8 @@ def tile_reverse_kl_backward_s8_kernel(
             if s < 4:
                 probs_to_psum(s + 1)
             e_turn(s)
-            if s < 3:
+            if s < 4:
                 hid_turn(2 + s // 2, s % 2, "d%d" % s)
-            if s == 1:
-                hid_turn(3, 1, "d3")
             if s in (1, 3):
                 voc_quant(s - 1)
             if s == 3:
@@ -538,8 +540,10 @@ def tile_reverse_kl_backward_s8_kernel(
             for c in range(3):
                 dhid_pass(1, x, c)
         hid_quant(3)
+        multiply_block(8, 0, nc.vector)
+        multiply(8, 0)
+        multiply_block(8, 1, nc.gpsimd)
         tok_quant(0, 0)
-        shared_multiply(8, nc.gpsimd)
         fill(5)
 
         subtract(18)
@@ -556,8 +560,10 @@ def tile_reverse_kl_backward_s8_kernel(
             for c in range(4):
                 dhid_pass(1, x, c)
         tok_quant(0, 1)
+        multiply_block(9, 0, nc.vector)
+        multiply(9, 0)
+        multiply_block(9, 1, nc.gpsimd)
         act_quant(0)
-        shared_multiply(9, nc.gpsimd)
         fill(2)
         dhid_out("S", 1, 2)
         dhid_out("S", 1, 3)

from contextlib import ExitStack

import concourse.mybir as mybir
from concourse.masks import make_identity

F32 = mybir.dt.float32
BF16 = mybir.dt.bfloat16
U32 = mybir.dt.uint32
I32 = mybir.dt.int32
U8 = mybir.dt.uint8
FP8 = mybir.dt.float8_e4m3fn
FP8X4 = mybir.dt.float8_e4m3fn_x4
FP4X4 = mybir.dt.float4_e2m1fn_x4
ALU = mybir.AluOpType
ACT = mybir.ActivationFunctionType

M, D, V, R = 1024, 1024, 2048, 512
P = 128
C = 512
FLOPS = 2 * M * D * V * 2 + 2 * M * R * V
RUN = 8
SHARE = (336, 352, 352, 352, 336)
Z3_FROM = 12
MOVED = ((False, False, True, True), (True,) * 4)
BLOCKS = [(0, 0, 1), (0, 1, 1), (0, 2, 2), (1, 0, 4)]
ORDER = [(j, c) for c in range(4) for j in (0, 1)] + [(j, c) for j in (2, 3) for c in range(4)]


def tile_reverse_kl_backward_s8_kernel(
    tc, hid, w_bytes, w_scale, teach, centre, probs, u_words, u_scales, act, out_0, out_1
):
    nc = tc.nc
    with ExitStack() as ctx:
        keep = ctx.enter_context(tc.tile_pool(name="keep", bufs=1))
        work = ctx.enter_context(tc.tile_pool(name="work", bufs=2))
        psum = ctx.enter_context(tc.psum_pool(name="psum", bufs=1))
        ctx.enter_context(tc.manual_schedule())

        wsc = keep.tile([P, 8], F32, name="wsc")
        cen = keep.tile([P, 8], BF16, name="cen")
        cen32 = keep.tile([P, 8], F32, name="cen32")
        ident = keep.tile([P, P], F32, name="ident")
        ident16 = keep.tile([P, P], BF16, name="ident16")
        u_codes = [keep.tile([P, 2 * D], U8, name="u_codes_%d" % c, align_bytes=64) for c in range(4)]
        u_sc = keep.tile([P, 4, D], U8, name="u_sc", align_bytes=64)

        def mx_tiles(pool, name, width, bufs):
            codes = pool.tile([P, width], U32, name=name + "_codes", align_bytes=64, bufs=bufs)
            scales = pool.tile([P, width], U8, name=name + "_scales", align_bytes=64, bufs=bufs)
            return codes, scales

        def quantise(mx, src, a, b):
            nc.vector.quantize_mx(out=mx[0][:, a:b].bitcast(FP8X4), scales=mx[1][:, a:b], in_=src[:, 4 * a : 4 * b])

        def bank(name):
            return psum.tile([P, C], F32, name=name)

        w_view = w_bytes.rearrange("(g p t) v -> g p t v", p=P, t=4)
        w_raw = {}

        def load_w(kg, c, n, pieces=1):
            wb = keep.tile([P, 4, n * C], U8, name="w_bytes_%d_%d" % (kg, c))
            for a in range(0, 4, 4 // pieces):
                planes = slice(a, a + 4 // pieces)
                nc.sync.dma_start(out=wb[:, planes], in_=w_view[kg][:, planes, c * C : (c + n) * C])
            for i in range(n):
                w_raw[kg, c + i] = wb[:, :, i * C : (i + 1) * C]

        def slots(src, j):
            g, h = divmod(j, 2)
            return src[g * C : (g + 1) * C, :].rearrange("(p t) x -> p t x", t=4)[:, 2 * h : 2 * h + 2, :]

        hid_rows = {}

        def load_hid(j):
            hid_rows[j] = work.tile([P, 2 * D], BF16, name="rows", bufs=4)
            nc.sync.dma_start(out=hid_rows[j][:].rearrange("p (t d) -> p t d", t=2), in_=slots(hid, j))

        act_rows = {}

        def load_act(g):
            act_rows[g] = work.tile([P, 4 * R], BF16, name="rows", bufs=4)
            nc.sync.dma_start(out=act_rows[g][:], in_=act[g * C : (g + 1) * C, :].rearrange("(p t) r -> p (t r)", t=4))

        tp = {}
        for g, c, n in BLOCKS:
            tile = keep.tile([P, 8 * n * C], BF16, name="tp_%d_%d" % (g, c))
            for i in range(n):
                tp[g, c + i] = tile[:].rearrange("p (x t v) -> p x t v", x=2, t=4)[:, :, :, i * C : (i + 1) * C]
            tp["block", g, c] = tile, n

        def load_tp(j, c):
            g, h = divmod(j, 2)
            tile, n = tp["block", g, c]
            for x, src in ((1, probs), (0, teach)) if g == 0 else ((0, teach), (1, probs)):
                a = (4 * x + 2 * h) * n * C
                nc.sync.dma_start(
                    out=tile[:, a : a + 2 * n * C].rearrange("p (t v) -> p t v", t=2),
                    in_=slots(src, j)[:, :, c * C : (c + n) * C],
                )

        def load_u(c):
            nc.sync.dma_start(out=u_codes[c][:], in_=u_words[c])

        def load_u_scales():
            for r in range(4):
                nc.sync.dma_start(
                    out=u_sc[r:P:32, :, :].bitcast(I32),
                    in_=u_scales[:, r:16:4, :].rearrange("g q n -> q g n").bitcast(I32),
                )

        wide = {}
        woven = {}

        def widen(k, engines, a=0, b=C):
            c, kg = divmod(k, 2)
            if k not in wide:
                wide[k] = work.tile([P, 4, C], BF16, name="wide", bufs=3)
            for t in range(4):
                src = w_raw[kg, c][:, t, a:b].bitcast(FP8)
                sc = wsc[:, 4 * kg + t : 4 * kg + t + 1]
                if engines[t] == "S":
                    nc.scalar.activation(out=wide[k][:, t, a:b], in_=src, func=ACT.Copy, scale=sc)
                elif engines[t] == "V":
                    nc.vector.tensor_scalar(out=wide[k][:, t, a:b], in0=src, scalar1=sc, scalar2=None, op0=ALU.mult)

        def weave(key, src, engine, a=0, b=C):
            if key not in woven:
                woven[key] = work.tile([P, 4 * C], BF16, name="woven", align_bytes=64, bufs=5)
            dst = woven[key][:, 4 * a : 4 * b]
            if engine == "G":
                nc.gpsimd.tensor_scalar(
                    out=dst.rearrange("p (c t) -> p c t", t=4),
                    in0=src[:, :, a:b].rearrange("p t c -> p c t"),
                    scalar1=1.0,
                    scalar2=0.0,
                    op0=ALU.mult,
                    op1=ALU.add,
                )
                return
            o = dst.rearrange("p (c i t) -> p c t i", i=RUN, t=4)
            s = src[:, :, a:b].rearrange("p t (c i) -> p c t i", i=RUN)
            if engine == "V":
                nc.vector.tensor_copy(out=o, in_=s)
            else:
                nc.scalar.copy(out=o, in_=s)

        w_mx = {k: mx_tiles(keep, "w_%d" % k, C, 1) for k in range(8)}
        hid_mx = {j: mx_tiles(keep, "hid_%d" % j, C, 1) for j in range(4)}
        act_mx = {g: mx_tiles(keep, "act_%d" % g, R, 1) for g in range(2)}

        def w_weave(k, engine, a=0, b=C):
            weave(("w", k), wide[k][:], engine, a, b)

        def w_quant(k, a=0, b=C):
            quantise(w_mx[k], woven["w", k], a, b)

        def turn(b, words):
            for i, w in enumerate(words):
                nc.tensor.transpose(b[:, i * P : (i + 1) * P], w, ident[:])

        def unturn(dst, b):
            nc.scalar.copy(
                out=dst.bitcast(F32).rearrange("q (t p u) -> q t p u", t=2, u=2),
                in_=b[:].rearrange("q (t u p) -> q t p u", t=2, u=2),
            )

        hid_t = {}
        turned = {}

        def hid_turn(j, kg, name):
            words = hid_rows[j][:].bitcast(F32)
            turned["hid", j, kg] = b = bank(name)
            turn(b, [words[:, t * C + kg * 2 * P + u : t * C + (kg + 1) * 2 * P : 2] for t in range(2) for u in range(2)])

        def hid_unturn(j, kg):
            if j not in hid_t:
                hid_t[j] = work.tile([P, 4 * C], BF16, name="hid_t", align_bytes=64, bufs=2)
            unturn(hid_t[j][:, kg * 2 * C : (kg + 1) * 2 * C], turned["hid", j, kg])

        def hid_quant(j):
            quantise(hid_mx[j], hid_t[j], 0, C)

        def where(s):
            j, c = ORDER[s]
            return j, c, j // 2, 2 * (j % 2)

        zb = {}

        def z_mm(n, parts=((0, 0, C), (1, 0, C))):
            s, i = divmod(n, 2)
            j, c, g, t = where(s)
            if n not in zb:
                zb[n] = bank("z%d" % (n % 2 if n < Z3_FROM else n % 3))
            for kg, a, b in parts:
                cols = slice((2 * kg + i) * P, (2 * kg + i + 1) * P)
                nc.tensor.matmul_mx(
                    out=zb[n][:, a:b],
                    lhsT=hid_mx[j][0][:, cols].bitcast(FP8X4),
                    lhsT_scale=hid_mx[j][1][:, cols],
                    rhs=w_mx[2 * c + kg][0][:, a:b].bitcast(FP8X4),
                    rhs_scale=w_mx[2 * c + kg][1][:, a:b],
                    start=kg == 0,
                    stop=kg == 1 and a == 0,
                )

        diff = {}

        def subtract(n):
            s, i = divmod(n, 2)
            j, c, g, t = where(s)
            if i == 0:
                diff[s] = work.tile([P, 2 * C], F32, name="diff", bufs=2)
            nc.vector.scalar_tensor_tensor(
                out=diff[s][:, i * C : (i + 1) * C],
                in0=zb[n][:],
                scalar=cen32[:, 4 * g + t + i : 4 * g + t + i + 1],
                in1=tp[g, c][:, 0, t + i, :],
                op0=ALU.subtract,
                op1=ALU.subtract,
            )

        def e_block(s, i, u):
            j, c, g, t = where(s)
            if i == 1 and u == 1 and MOVED[g][c]:
                return tp[g, c][:, 1, t, 2 * P :]
            return tp[g, c][:, 0, t + i, u * 2 * P : (u + 1) * 2 * P]

        probs_bank = {}

        def probs_to_psum(s):
            j, c, g, t = where(s)
            probs_bank[s] = b = psum.tile([P, 2 * C], BF16, name="z2")
            for i in range(2):
                nc.tensor.matmul(
                    out=b[:, i * C : (i + 1) * C], lhsT=ident16[:], rhs=tp[g, c][:, 1, t + i, :], start=True, stop=True
                )

        def factors(s, i):
            j, c, g, t = where(s)
            p = probs_bank[s][:, i * C : (i + 1) * C] if s in probs_bank else tp[g, c][:, 1, t + i, :]
            view = "p (x u e) -> p u x e"
            return diff[s][:, i * C : (i + 1) * C].rearrange(view, u=2, e=2), p.rearrange(view, u=2, e=2)

        def multiply(s, i):
            j, c, g, t = where(s)
            d, p = factors(s, i)
            if i == 1 and MOVED[g][c]:
                nc.vector.tensor_tensor(out=e_block(s, 1, 0), in0=d[:, 0], in1=p[:, 0], op=ALU.mult)
                nc.vector.tensor_tensor(out=e_block(s, 1, 1), in0=d[:, 1], in1=p[:, 1], op=ALU.mult)
                return
            nc.vector.tensor_tensor(out=tp[g, c][:, 0, t + i, :], in0=d, in1=p, op=ALU.mult)

        def multiply_block(s, u, engine, i=1):
            d, p = factors(s, i)
            engine.tensor_tensor(out=e_block(s, i, u), in0=d[:, u], in1=p[:, u], op=ALU.mult)

        e_t = {}
        voc_mx = {}

        def e_turn(s, name="t0"):
            turned["e", s] = b = bank(name)
            turn(b, [e_block(s, i, u).bitcast(F32) for i in range(2) for u in range(2)])

        def e_unturn(s):
            e_t[s] = work.tile([P, 2 * C], BF16, name="e_t", align_bytes=64, bufs=5)
            unturn(e_t[s][:], turned["e", s])

        def voc_quant(s):
            voc_mx[ORDER[s]] = mx_tiles(work, "voc", 2 * P, 6)
            quantise(voc_mx[ORDER[s]], e_t[s], 0, 2 * P)

        held = {}

        def dhid_pass(j, x, c, name=None, a=0, b=C):
            i, nh = divmod(x, 2)
            if c == 0:
                held[j, x, a] = bank(name or "d%d" % x)
            n0 = nh * C
            nc.tensor.matmul_mx(
                out=held[j, x, a][:, : b - a],
                lhsT=voc_mx[j, c][0][:, i * P : (i + 1) * P].bitcast(FP8X4),
                lhsT_scale=voc_mx[j, c][1][:, i * P : (i + 1) * P],
                rhs=u_codes[c][:, 2 * (n0 + a) : 2 * (n0 + b)].bitcast(FP4X4),
                rhs_scale=u_sc[:, c, n0 + a : n0 + b],
                start=c == 0,
                stop=c == 3,
            )

        def copy_out(engine, src, dst, shape, width=C):
            if engine == "S":
                r = work.tile([P, width], F32, name="res", bufs=6)
                nc.scalar.copy(out=shape(r[:]), in_=src)
            else:
                r = work.tile([P, width], F32, name="rows", bufs=4)
                nc.vector.tensor_copy(out=shape(r[:]), in_=src)
            nc.sync.dma_start(out=dst, in_=r[:])

        def dhid_out(engine, j, x, a=0, b=C):
            i, nh = divmod(x, 2)
            copy_out(engine, held[j, x, a][:, : b - a], slots(out_0, j)[:, i, nh * C + a : nh * C + b], lambda r: r, b - a)

        tok_mx = {}

        def tok_weave(g, c, engine, a=0, b=C):
            key = ("tok", g, c)
            if not MOVED[g][c]:
                weave(key, tp[g, c][:, 0], engine, a, b)
                return
            if a < 2 * P:
                weave(key, tp[g, c][:, 0], engine, a, min(b, 2 * P))
            if b > 2 * P:
                a = max(a, 2 * P)
                if key not in woven:
                    woven[key] = work.tile([P, 4 * C], BF16, name="woven", align_bytes=64, bufs=5)
                src = tp[g, c][:, :, 0:4:2, a:b].rearrange("p e h (c i) -> p c h e i", i=RUN)
                o = woven[key][:, 4 * a : 4 * b].rearrange("p (c i h e) -> p c h e i", i=RUN, h=2, e=2)
                if engine == "V":
                    nc.vector.tensor_copy(out=o, in_=src)
                else:
                    nc.scalar.copy(out=o, in_=src)

        def tok_quant(g, c):
            tok_mx[g, c] = mx_tiles(work, "tok", C, 6)
            quantise(tok_mx[g, c], woven["tok", g, c], 0, C)

        def act_weave(g, engine, a=0, b=R):
            weave(("act", g), act_rows[g][:].rearrange("p (t r) -> p t r", t=4), engine, a, b)

        def act_quant(g):
            quantise(act_mx[g], woven["act", g], 0, R)

        dup_b = {}

        def dup(name, r, c):
            dup_b[r, c] = b = bank(name)
            for g in range(2):
                nc.tensor.matmul_mx(
                    out=b[:],
                    lhsT=act_mx[g][0][:, r * P : (r + 1) * P].bitcast(FP8X4),
                    lhsT_scale=act_mx[g][1][:, r * P : (r + 1) * P],
                    rhs=tok_mx[g, c][0][:].bitcast(FP8X4),
                    rhs_scale=tok_mx[g, c][1][:],
                    start=g == 0,
                    stop=g == 1,
                )

        def dup_out(engine, r, c):
            copy_out(
                engine,
                dup_b[r, c][:].rearrange("p (u q e) -> p q u e", u=2, e=2),
                out_1[r * P : (r + 1) * P, c * C : (c + 1) * C],
                lambda x: x.rearrange("p (q u e) -> p q u e", u=2, e=2),
            )

        nc.scalar.dma_start(
            out=wsc[:].rearrange("p (g t) -> p g t", t=4), in_=w_scale.rearrange("(g p t) o -> p g (t o)", p=P, t=4)
        )
        nc.scalar.dma_start(out=cen[:].rearrange("p (g t) -> p g t", t=4), in_=centre.rearrange("(g p t) -> p g t", p=P, t=4))
        nc.scalar.activation(out=cen32[:], in_=cen[:], func=ACT.Copy)
        make_identity(nc, ident[:])
        nc.scalar.copy(out=ident16[:], in_=ident[:])
        nc.vector.memset(u_sc[:].rearrange("p g n -> p (g n)").bitcast(I32), 0)

        load_w(0, 0, 1)
        load_w(1, 0, 1)
        load_hid(0)
        load_w(0, 1, 1)
        load_hid(1)
        load_w(1, 1, 1)
        load_tp(0, 0)
        load_w(0, 2, 2)
        load_tp(1, 0)
        load_w(1, 2, 2)
        load_hid(2)
        load_tp(0, 1)
        load_hid(3)
        load_tp(1, 1)
        load_u_scales()
        load_u(0)
        load_tp(0, 2)
        load_u(1)
        load_tp(1, 2)
        load_u(2)
        load_u(3)
        load_act(0)
        load_act(1)
        load_tp(2, 0)
        load_tp(3, 0)

        hid_turn(0, 0, "d0")
        hid_turn(0, 1, "d1")
        widen(0, "VVVS")
        widen(1, "VVSS")
        w_weave(0, "V", 0, C - P)
        w_weave(0, "S", C - P, C)
        w_weave(1, "V")
        widen(2, "S---")
        hid_unturn(0, 0)
        widen(2, "-S--")
        hid_unturn(0, 1)
        widen(2, "--S-")
        w_quant(0)
        w_quant(1)
        widen(2, "---V")
        widen(3, "V---")
        hid_quant(0)
        hid_turn(1, 0, "d2")
        hid_turn(1, 1, "d3")
        z_mm(0)
        z_mm(1)
        probs_to_psum(0)
        w_weave(2, "V", 0, C - 96)

        PIECE = 384

        def gate(k):
            widen(k, "---V", 0, PIECE)
            w_weave(k, "G", 0, SHARE[k - 3])

        def passes(j, c, xs=range(4)):
            for x in xs:
                dhid_pass(j, x, c)

        def shared_multiply(s, engine):
            multiply(s, 0)
            multiply_block(s, 1, engine)
            multiply_block(s, 0, nc.vector)

        hid_unturn(1, 0)
        hid_unturn(1, 1)
        w_weave(2, "S", C - 96, C)
        widen(3, "---S", PIECE, C)
        widen(3, "-SS-")
        hid_quant(1)
        gate(3)
        w_quant(2)

        quarters = [(tok_weave, (0, c), q) for c in range(2) for q in range(4)]
        quarters = quarters + [(act_weave, (g,), q) for g in range(2) for q in range(4)]
        quarters = quarters + [(tok_weave, (0, c), q) for c in (2, 3) for q in range(4)]
        filled = []

        def fill(n):
            for f, key, q in quarters[len(filled) : len(filled) + n]:
                f(*key, "S", q * P, (q + 1) * P)
                filled.append(q)

        for s in range(5):
            k = s + 3
            subtract(2 * s)
            z_mm(2 * s + 2)
            subtract(2 * s + 1)
            z_mm(2 * s + 3)
            if s < 4:
                widen(k + 1, "S---")
            else:
                hid_unturn(3, 0)
            w_weave(k, "S", SHARE[s], C)
            if s > 0:
                e_unturn(s - 1)
            if s < 4:
                widen(k + 1, "---S", PIECE, C)
                widen(k + 1, "-SS-")
            else:
                hid_unturn(3, 1)
            if s in (1, 3):
                hid_unturn(2, s // 2)
            if s == 3:
                passes(0, 0, (0,))
            if s == 4:
                passes(0, 0, (1,))
                passes(0, 1, (1,))
                passes(0, 0, (2,))
            multiply(s, 0)
            multiply(s, 1)
            if s < 4:
                probs_to_psum(s + 1)
            e_turn(s)
            if s < 4:
                hid_turn(2 + s // 2, s % 2, "d%d" % s)
            if s in (1, 3):
                voc_quant(s - 1)
            if s == 3:
                passes(0, 1, (0,))
            if s < 4:
                gate(k + 1)
            w_quant(k)

        passes(0, 1, (2,))
        passes(0, 0, (3,))
        fill(2)
        e_unturn(4)
        fill(5)

        subtract(10)
        z_mm(12)
        subtract(11)
        z_mm(13)
        passes(0, 1, (3,))
        hid_quant(2)
        voc_quant(4)
        passes(0, 2)
        shared_multiply(5, nc.gpsimd)

        z_mm(14)
        subtract(12)
        z_mm(15)
        subtract(13)
        multiply(6, 0)
        multiply(6, 1)
        e_turn(6)
        z_mm(16)
        fill(2)
        e_unturn(6)
        fill(2)

        subtract(14)
        z_mm(17)
        subtract(15)
        e_turn(5)
        e_unturn(5)
        voc_quant(1)
        voc_quant(3)
        voc_quant(6)
        passes(0, 3)
        z_mm(18)
        shared_multiply(7, nc.gpsimd)
        for x in range(4):
            dhid_out("S", 0, x)

        subtract(16)
        z_mm(19)
        subtract(17)
        voc_quant(5)
        e_turn(7)
        e_unturn(7)
        z_mm(20)
        for x in range(2):
            for c in range(3):
                dhid_pass(1, x, c)
        hid_quant(3)
        multiply_block(8, 0, nc.vector)
        multiply(8, 0)
        multiply_block(8, 1, nc.gpsimd)
        tok_quant(0, 0)
        fill(5)

        subtract(18)
        subtract(19)
        voc_quant(7)
        z_mm(21)
        z_mm(22)
        passes(1, 3, range(2))
        e_turn(8)
        dhid_out("S", 1, 0)
        dhid_out("S", 1, 1)
        e_unturn(8)
        for x in range(2, 4):
            for c in range(4):
                dhid_pass(1, x, c)
        tok_quant(0, 1)
        multiply_block(9, 0, nc.vector)
        multiply(9, 0)
        multiply_block(9, 1, nc.gpsimd)
        act_quant(0)
        fill(2)
        dhid_out("S", 1, 2)
        dhid_out("S", 1, 3)
        fill(1)

        subtract(20)
        subtract(21)
        z_mm(23)
        z_mm(24)
        e_turn(9)
        e_unturn(9)
        act_quant(1)
        voc_quant(8)
        passes(2, 0)
        shared_multiply(10, nc.gpsimd)
        fill(3)

        subtract(22)
        subtract(23)
        z_mm(25)
        z_mm(26)
        e_turn(10)
        fill(1)
        e_unturn(10)
        fill(1)
        multiply_block(11, 1, nc.vector, 0)
        multiply_block(11, 0, nc.vector)
        voc_quant(9)
        passes(2, 1)
        multiply_block(11, 0, nc.vector, 0)
        multiply_block(11, 1, nc.gpsimd)
        tok_quant(0, 2)

        subtract(24)
        subtract(25)
        e_turn(11)
        e_unturn(11)
        z_mm(27)
        z_mm(28)
        multiply_block(12, 1, nc.vector, 0)
        voc_quant(10)
        passes(2, 2)
        multiply_block(12, 0, nc.vector)
        tok_quant(0, 3)
        multiply_block(12, 0, nc.vector, 0)
        multiply_block(12, 1, nc.gpsimd)
        voc_quant(11)
        passes(2, 3)
        tok_weave(1, 0, "S", 0, C // 2)

        subtract(26)
        subtract(27)
        tok_weave(1, 0, "V", C // 2, C)
        multiply_block(13, 0, nc.vector)
        tok_quant(1, 0)
        z_mm(29)
        z_mm(30)
        for x in range(4):
            dhid_out("S", 2, x)
        for r in range(4):
            dup("d%d" % r, r, 0)
        multiply(13, 0)
        multiply_block(13, 1, nc.gpsimd)
        tok_weave(1, 1, "S", 0, C // 2)
        for r in range(4):
            dup_out("S", r, 0)

        subtract(28)
        subtract(29)
        multiply_block(14, 1, nc.vector, 0)
        tok_weave(1, 1, "V", C // 2, C)
        multiply_block(14, 0, nc.vector)
        multiply_block(14, 0, nc.vector, 0)
        tok_quant(1, 1)
        z_mm(31)
        e_turn(12, "z2")
        e_turn(13)
        e_unturn(12)
        e_unturn(13)
        for r in range(4):
            dup("d%d" % r, r, 1)
            dup_out("S", r, 1)
        multiply_block(14, 1, nc.vector)
        e_turn(14)
        e_unturn(14)
        tok_weave(1, 2, "V")
        voc_quant(12)
        tok_quant(1, 2)
        voc_quant(13)
        dhid_pass(3, 0, 0, "z2")
        dhid_pass(3, 0, 1)

        subtract(30)
        subtract(31)
        for r in range(3):
            dup("d%d" % r, r, 2)
        dup_out("S", 0, 2)
        dup_out("S", 1, 2)
        multiply(15, 0)
        multiply_block(15, 0, nc.vector)
        voc_quant(14)
        multiply_block(15, 1, nc.vector)
        e_turn(15)
        e_unturn(15)
        dup("d3", 3, 2)
        dup_out("S", 2, 2)
        dup_out("S", 3, 2)
        dhid_pass(3, 0, 2)
        for c in range(3):
            dhid_pass(3, 1, c, "z0")
        tok_weave(1, 3, "V")
        voc_quant(15)
        tok_quant(1, 3)
        dhid_pass(3, 0, 3)
        dhid_pass(3, 1, 3)
        dhid_out("S", 3, 0)
        dhid_out("V", 3, 1)
        for r in range(4):
            dup(("d1", "d2", "d3", "t0")[r], r, 3)
            dup_out("SV"[r % 2], r, 3)
        for c in range(4):
            dhid_pass(3, 2, c, "z1")
        dhid_out("S", 3, 2)
        for a, name, engine in ((0, "d0", "V"), (C // 2, "z2", "S")):
            for c in range(4):
                dhid_pass(3, 3, c, name, a, a + C // 2)
            dhid_out(engine, 3, 3, a, a + C // 2)
